import numpy as np
import ml_dtypes


def mxq(x, axis, fmt="e4m3"):
    dtype, down = {"e4m3": (ml_dtypes.float8_e4m3fn, 7), "e5m2": (ml_dtypes.float8_e5m2, 14)}[fmt]
    v = np.moveaxis(np.asarray(x, np.float32).astype(ml_dtypes.bfloat16).astype(np.float64), axis, -1)
    blocks = v.reshape(v.shape[:-1] + (-1, 32))
    amax = np.abs(blocks).max(-1, keepdims=True)
    byte = np.maximum(np.where(amax > 0, np.frexp(amax)[1] - 1 + 127, 0) - down, 1)
    scale = np.exp2(byte - 127.0)
    codes = (blocks / scale).astype(np.float32).astype(dtype).astype(np.float64)
    return np.moveaxis((codes * scale).reshape(v.shape), -1, axis)


WIDE = False


def mx_kscale(k):
    if not WIDE:
        return np.ones(k)
    levels = np.array([10, -10, 5, -5, 0])
    if k % 512:
        return np.exp2(np.random.permutation(np.resize(levels, k // 32))).repeat(32)
    a = np.empty((k // 512, 16))
    for p in range(k // 512):
        a[p, :8] = np.random.permutation(np.resize(levels, 8))
        for g in range(8):
            far = levels[np.abs(levels - a[p, g]) >= 10]
            a[p, g + 8] = far[np.random.randint(len(far))]
    return np.exp2(a.ravel()).repeat(32)


BF16 = ml_dtypes.bfloat16


def bf(x):
    return np.asarray(x, np.float32).astype(BF16)


def f64(x):
    return np.asarray(x).astype(np.float64)

def planes(Y):
    n, m = Y.shape
    b = f64(bf(Y)).reshape(n // 32, 32, m)
    amax = np.abs(b).max(1)
    byte = np.clip(np.where(amax > 0, np.frexp(amax)[1] - 1 + 127 - 7, 1), 1, 254)
    codes = (b * np.exp2(127.0 - byte)[:, None, :]).reshape(n, m).astype(np.float32).astype(ml_dtypes.float8_e4m3fn).view(np.uint8)
    words = codes.reshape(n // 512, 128, 4, m).transpose(0, 1, 3, 2)
    return np.ascontiguousarray(words), np.ascontiguousarray(byte.astype(np.uint8).reshape(n // 512, 16, m))


T, N, O = 2, 1024, 512


def setup_inputs():
    u, v = mx_kscale(O), mx_kscale(N)
    return {"l": bf(np.random.standard_normal((T, N, O)) * u),
            "r": bf(np.random.standard_normal((T, N, O)) * (2.0 / T) ** 0.25 / np.sqrt(O) / u * v[None, :, None]),
            "occ": bf(np.random.uniform(0.5, 1.5, (T, O))),
            "s": bf(np.random.standard_normal((N, N)) / np.sqrt(N) / v[:, None])}


def spin_density(l, r, occ):
    ln = l * occ[:, None, :]
    return mxq(ln, 2, "e4m3") @ mxq(r, 2, "e4m3").transpose(0, 2, 1)


def core(l, r, occ, s):
    p = spin_density(f64(l), f64(r), f64(occ))
    ps = mxq(p, 2, "e4m3") @ mxq(f64(s), 0, "e4m3")
    e = ps * np.swapaxes(ps, -1, -2)
    return 2.0 * np.sum(e, axis=0)


def reference(l, r, occ, s):
    R_out = core(l, r, occ, s)
    words, scales = planes(R_out.T)
    return R_out, words, scales

@@ -1,0 +1,491 @@
+from contextlib import ExitStack
+
+import concourse.mybir as mybir
+from concourse.masks import make_identity
+
+T, N, O = 2, 1024, 512
+FLOPS = 2 * T * (N * N * O + N * N * N)
+
+F32 = mybir.dt.float32
+BF16 = mybir.dt.bfloat16
+U32 = mybir.dt.uint32
+I32 = mybir.dt.int32
+U8 = mybir.dt.uint8
+FP8X4 = mybir.dt.float8_e4m3fn_x4
+MULT = mybir.AluOpType.mult
+ADD = mybir.AluOpType.add
+
+P = 128
+PACK = 4
+GROUP = P * PACK
+G = N // GROUP
+
+
+def tile_biorthogonalspinmayerbondorder_x1_kernel(tc, l, r, occ, s, out_0, out_1, out_2):
+    nc = tc.nc
+    with ExitStack() as ctx:
+        keep = ctx.enter_context(tc.tile_pool(name="keep", bufs=1))
+        work = ctx.enter_context(tc.tile_pool(name="work", bufs=4))
+        psum = ctx.enter_context(tc.psum_pool(name="psum", bufs=8))
+        ctx.enter_context(tc.manual_schedule())
+
+        raw, staged, quantised, banks, products, result = {}, {}, {}, {}, {}, {}
+
+        def bank(key):
+            banks[key] = psum.tile([P, GROUP], F32, name="bank")
+            return banks[key]
+
+        def copier(engine):
+            return nc.scalar.copy if engine == "act" else nc.vector.tensor_copy
+
+        def load_orbitals(which, t, g, j0, step):
+            src = (l if which == "l" else r)[t, g * GROUP : (g + 1) * GROUP, :].rearrange("(m j) k -> m j k", j=PACK)
+            piece = keep.tile([P, step, O], BF16, name="raw_%s%d%d%d" % (which, t, g, j0))
+            nc.sync.dma_start(out=piece[:], in_=src[:, j0 : j0 + step, :])
+            for j in range(step):
+                raw[which, t, g, j0 + j] = piece[:, j, :]
+
+        def load_overlap(h, g):
+            piece = keep.tile([P, PACK, GROUP], BF16, name="raw_s%d%d" % (h, g))
+            src = s[h * GROUP : (h + 1) * GROUP, g * GROUP : (g + 1) * GROUP]
+            nc.sync.dma_start(out=piece[:], in_=src.rearrange("(p j) d -> p j d", j=PACK))
+            raw["s", h, g] = piece
+
+        def stage(key):
+            if key not in staged:
+                staged[key] = work.tile([P, GROUP * PACK], BF16, name="staged", align_bytes=64, bufs=9)
+            return staged[key]
+
+        def turn(which, t, g, half):
+            dst = bank((which, t, g, half))
+            for j2 in range(2):
+                words = raw[which, t, g, 2 * half + j2].bitcast(F32)
+                for u in range(2):
+                    at = (2 * u + j2) * P
+                    nc.tensor.transpose(dst[:, at : at + P], words[:, u::2], ident[:])
+
+        def turn_out(which, t, g, half, engine):
+            src = banks[which, t, g, half]
+            dst = stage((which, t, g))[:, half * 2 * GROUP : (half + 1) * 2 * GROUP]
+            if which == "r":
+                copier(engine)(
+                    out=dst.bitcast(F32).rearrange("p (c u) -> p c u", u=2),
+                    in_=src[:].rearrange("p (u c) -> p c u", u=2),
+                )
+            else:
+                nc.vector.tensor_tensor(
+                    out=dst.rearrange("p (c u e) -> p c u e", u=2, e=2),
+                    in0=src[:].bitcast(BF16).rearrange("p (u c e) -> p c u e", u=2, e=2),
+                    in1=occ_sb[:, t, :].rearrange("p (u e) -> p u e", u=2).unsqueeze(1).to_broadcast([P, 2 * P, 2, 2]),
+                    op=MULT,
+                )
+
+        def quantise(key):
+            name = "_".join(str(part) for part in key)
+            codes = keep.tile([P, GROUP], U32, name="codes_" + name, align_bytes=64)
+            scales = keep.tile([P, GROUP], U8, name="scales_" + name, align_bytes=64)
+            nc.vector.quantize_mx(out=codes[:].bitcast(FP8X4), scales=scales[:], in_=staged[key][:])
+            quantised[key] = (codes, scales)
+
+        def mx(dst, left, left_cols, right, right_cols, start, stop):
+            nc.tensor.matmul_mx(
+                out=dst,
+                lhsT=quantised[left][0][:, left_cols].bitcast(FP8X4),
+                lhsT_scale=quantised[left][1][:, left_cols],
+                rhs=quantised[right][0][:, right_cols].bitcast(FP8X4),
+                rhs_scale=quantised[right][1][:, right_cols],
+                start=start,
+                stop=stop,
+            )
+
+        def block(j, count=1):
+            return slice(j * P, (j + count) * P)
+
+        def density(t, h, g, c):
+            dst = bank(("p", t, h, g, c))
+            for j in range(PACK):
+                mx(dst[:, block(j)], ("r", t, h), block(j), ("l", t, g), block(c), True, True)
+
+        def density_out(t, h, g, c, engine):
+            dst = stage(("p", t, h, g))[:, c * GROUP : (c + 1) * GROUP]
+            copier(engine)(
+                out=dst.rearrange("p (m j) -> p m j", j=PACK),
+                in_=banks["p", t, h, g, c][:].rearrange("p (j m) -> p m j", j=PACK),
+            )
+
+        def overlap_interleave(h, g, half, engine):
+            c = slice(2 * half, 2 * half + 2)
+            copier(engine)(
+                out=stage(("s", h, g))[:].rearrange("p (c q j) -> p c q j", c=PACK, j=PACK)[:, c],
+                in_=raw["s", h, g][:].rearrange("p j (q c) -> p c q j", c=PACK)[:, c],
+            )
+
+        def pieces_of(unit):
+            g, g2, j = unit
+            if g == g2 and j == 2:
+                return [(2, block(0, 2), block(2, 2)), (3, block(2, 2), block(2, 2))]
+            return [(j, block(0, 4), block(0, 4))]
+
+        def direct_product(t, unit):
+            g, g2, _ = unit
+            direct = bank(("x", t, unit))
+            for j, at, cols in pieces_of(unit):
+                for h in range(G):
+                    mx(direct[:, at], ("p", t, h, g), block(j), ("s", h, g2), cols, h == 0, h == G - 1)
+
+        def mirror_product(t, unit):
+            g, g2, _ = unit
+            mirror = bank(("y", t, unit))
+            for j, at, cols in pieces_of(unit):
+                for h in range(G):
+                    mx(mirror[:, at], ("s", h, g), block(j), ("p", t, h, g2), cols, h == 0, h == G - 1)
+
+        def direct_out(t, unit):
+            staged["x", t, unit] = work.tile([P, GROUP], F32, name="direct", bufs=6)
+            nc.scalar.copy(out=staged["x", t, unit][:], in_=banks["x", t, unit][:])
+
+        def multiply(t, unit):
+            products[t, unit] = keep.tile([P, GROUP], F32, name="product_%d_%d%d%d" % ((t,) + unit))
+            nc.vector.scalar_tensor_tensor(
+                out=products[t, unit][:], in0=banks["y", t, unit][:], scalar=2.0, in1=staged["x", t, unit][:], op0=MULT, op1=MULT
+            )
+
+        def quadrant(g, g2):
+            if (g, g2) not in result:
+                result[g, g2] = keep.tile([P, PACK, GROUP], F32, name="result_%d%d" % (g, g2))
+            return result[g, g2]
+
+        def add_channels(unit, engine="dve"):
+            g, g2, j = unit
+            (nc.vector if engine == "dve" else nc.gpsimd).tensor_tensor(
+                out=quadrant(g, g2)[:, j, :].rearrange("p (q c) -> p q c", c=PACK),
+                in0=products[0, unit][:].rearrange("p (c q) -> p q c", c=PACK),
+                in1=products[1, unit][:].rearrange("p (c q) -> p q c", c=PACK),
+                op=ADD,
+            )
+
+        def mirror_rows(g, g2, j):
+            dst = bank(("m", g, g2, j))
+            for c in range(PACK):
+                for t in range(T):
+                    if g == g2 and c >= 2:
+                        src = products[t, (g, g, 2)][:, block(2 * (c - 2) + j - 2)]
+                    else:
+                        src = products[t, (g2, g, c)][:, block(j)]
+                    nc.tensor.matmul(out=dst[:, block(c)], lhsT=src, rhs=ident[:], start=t == 0, stop=t == T - 1, is_transpose=True)
+
+        def mirror_out(g, g2, j, engine="act"):
+            copier(engine)(
+                out=quadrant(g, g2)[:, j, :].rearrange("p (q c) -> p q c", c=PACK),
+                in_=banks["m", g, g2, j][:].rearrange("p (c q) -> p q c", c=PACK),
+            )
+
+        def store_rows(g, g2, j0, count):
+            rows = out_0[g * GROUP : (g + 1) * GROUP, g2 * GROUP : (g2 + 1) * GROUP].rearrange("(p j) m -> p j m", j=PACK)
+            nc.sync.dma_start(out=rows[:, j0 : j0 + count, :], in_=result[g, g2][:, j0 : j0 + count, :])
+
+        def round_result(g, g2, half, engine):
+            m = slice(half * 2 * P, (half + 1) * 2 * P)
+            copier(engine)(
+                out=stage(("o", g, g2))[:].rearrange("p (m j) -> p m j", j=PACK)[:, m, :],
+                in_=result[g, g2][:].rearrange("p j m -> p m j")[:, m, :],
+            )
+
+        def quantise_result(g, g2):
+            cols = slice(g2 * GROUP, (g2 + 1) * GROUP)
+            codes = keep.tile([P, GROUP], U32, name="out_codes_%d%d" % (g, g2), align_bytes=64)
+            nc.vector.quantize_mx(out=codes[:].bitcast(FP8X4), scales=out_scales[g][:, cols], in_=staged["o", g, g2][:])
+            quantised["o", g, g2] = codes
+
+        def store_words(g, g2):
+            words = out_1[g].rearrange("p m j -> p (m j)").bitcast(I32)
+            nc.sync.dma_start(out=words[:, g2 * GROUP : (g2 + 1) * GROUP], in_=quantised["o", g, g2][:].bitcast(I32))
+
+        def store_scales(g):
+            for q in range(4):
+                nc.sync.dma_start(
+                    out=out_2[g, 4 * q : 4 * q + 4, :].bitcast(I32), in_=out_scales[g][32 * q : 32 * q + 4, :].bitcast(I32)
+                )
+
+        ident = keep.tile([P, P], F32, name="ident")
+        make_identity(nc, ident[:])
+        occ_sb = keep.tile([P, T, PACK], BF16, name="occ_sb")
+        nc.scalar.dma_start(out=occ_sb[:], in_=occ.rearrange("t (p j) -> p t j", j=PACK))
+        out_scales = [keep.tile([P, N], U8, name="out_scales_%d" % g, align_bytes=64) for g in range(G)]
+
+        load_orbitals('l', 0, 0, 0, 2)
+        load_orbitals('l', 0, 0, 2, 2)
+        turn('l', 0, 0, 0)
+        turn('l', 0, 0, 1)
+        load_orbitals('r', 0, 0, 2, 2)
+        load_orbitals('r', 0, 0, 0, 2)
+        turn('r', 0, 0, 1)
+        turn_out('r', 0, 0, 1, 'act')
+        turn('r', 0, 0, 0)
+        load_orbitals('r', 0, 1, 0, 4)
+        turn_out('l', 0, 0, 0, 'act')
+        turn('r', 0, 1, 0)
+        turn_out('r', 0, 1, 0, 'act')
+        load_orbitals('r', 1, 0, 0, 4)
+        load_overlap(0, 0)
+        turn('r', 0, 1, 1)
+        turn_out('l', 0, 0, 1, 'act')
+        turn_out('r', 0, 0, 0, 'dve')
+        turn_out('r', 0, 1, 1, 'act')
+        quantise(('l', 0, 0))
+        quantise(('r', 0, 0))
+        overlap_interleave(0, 0, 1, 'act')
+        turn('r', 1, 0, 0)
+        density(0, 0, 0, 3)
+        load_orbitals('l', 1, 0, 0, 4)
+        density(0, 0, 0, 1)
+        turn('r', 1, 0, 1)
+        load_orbitals('r', 1, 1, 0, 4)
+        load_overlap(1, 0)
+        turn('l', 1, 0, 1)
+        turn('l', 1, 0, 0)
+        overlap_interleave(0, 0, 0, 'act')
+        turn_out('r', 1, 0, 1, 'act')
+        turn_out('r', 1, 0, 0, 'dve')
+        load_orbitals('l', 0, 1, 0, 4)
+        turn('r', 1, 1, 1)
+        quantise(('r', 0, 1))
+        density_out(0, 0, 0, 1, 'dve')
+        turn('r', 1, 1, 0)
+        density(0, 1, 0, 0)
+        density_out(0, 0, 0, 3, 'dve')
+        turn_out('l', 1, 0, 1, 'act')
+        density(0, 1, 0, 2)
+        turn_out('r', 1, 1, 1, 'act')
+        density(0, 0, 0, 2)
+        turn_out('l', 1, 0, 0, 'act')
+        turn('l', 0, 1, 0)
+        turn('l', 0, 1, 1)
+        overlap_interleave(1, 0, 0, 'act')
+        overlap_interleave(1, 0, 1, 'dve')
+        density(0, 0, 0, 0)
+        density_out(0, 1, 0, 0, 'act')
+        density_out(0, 0, 0, 2, 'act')
+        quantise(('r', 1, 0))
+        density(0, 1, 0, 3)
+        density_out(0, 1, 0, 2, 'act')
+        turn_out('r', 1, 1, 0, 'dve')
+        density_out(0, 1, 0, 3, 'act')
+        quantise(('l', 1, 0))
+        density(1, 0, 0, 0)
+        density(1, 0, 0, 2)
+        quantise(('r', 1, 1))
+        load_orbitals('l', 1, 1, 0, 4)
+        density(0, 1, 0, 1)
+        density_out(0, 0, 0, 0, 'act')
+        load_overlap(1, 1)
+        density(1, 1, 0, 3)
+        turn_out('l', 0, 1, 0, 'act')
+        density_out(1, 0, 0, 0, 'act')
+        density(1, 0, 0, 3)
+        turn_out('l', 0, 1, 1, 'act')
+        density_out(1, 0, 0, 3, 'act')
+        density(1, 0, 0, 1)
+        turn('l', 1, 1, 0)
+        density(1, 1, 0, 2)
+        density_out(1, 0, 0, 2, 'dve')
+        quantise(('l', 0, 1))
+        density_out(0, 1, 0, 1, 'act')
+        density(0, 0, 1, 0)
+        quantise(('s', 1, 0))
+        turn('l', 1, 1, 1)
+        density_out(1, 1, 0, 3, 'act')
+        density(0, 0, 1, 2)
+        density_out(1, 0, 0, 1, 'act')
+        quantise(('p', 0, 0, 0))
+        density(1, 1, 0, 0)
+        density_out(1, 1, 0, 2, 'act')
+        turn_out('l', 1, 1, 0, 'act')
+        quantise(('p', 0, 1, 0))
+        density(0, 1, 1, 1)
+        quantise(('s', 0, 0))
+        density(1, 1, 0, 1)
+        turn_out('l', 1, 1, 1, 'act')
+        density_out(0, 0, 1, 0, 'act')
+        density_out(1, 1, 0, 1, 'dve')
+        density_out(0, 0, 1, 2, 'act')
+        density(0, 1, 1, 0)
+        density_out(1, 1, 0, 0, 'act')
+        density(0, 0, 1, 3)
+        density_out(0, 0, 1, 3, 'dve')
+        quantise(('p', 1, 1, 0))
+        direct_product(0, (0, 0, 0))
+        density_out(0, 1, 1, 1, 'act')
+        density_out(0, 1, 1, 0, 'act')
+        density(0, 1, 1, 3)
+        direct_product(0, (0, 0, 1))
+        direct_product(0, (0, 0, 2))
+        direct_out(0, (0, 0, 0))
+        load_overlap(0, 1)
+        mirror_product(0, (0, 0, 0))
+        density_out(0, 1, 1, 3, 'act')
+        quantise(('l', 1, 1))
+        density(0, 1, 1, 2)
+        density(1, 0, 1, 0)
+        density(1, 1, 1, 2)
+        quantise(('p', 1, 0, 0))
+        direct_product(1, (0, 0, 1))
+        direct_out(0, (0, 0, 1))
+        overlap_interleave(1, 1, 0, 'dve')
+        direct_product(1, (0, 0, 0))
+        direct_out(0, (0, 0, 2))
+        density_out(1, 0, 1, 0, 'act')
+        mirror_product(0, (0, 0, 1))
+        density(1, 0, 1, 1)
+        density_out(1, 1, 1, 2, 'act')
+        multiply(0, (0, 0, 0))
+        direct_out(1, (0, 0, 0))
+        density(1, 0, 1, 2)
+        density_out(0, 1, 1, 2, 'dve')
+        overlap_interleave(1, 1, 1, 'dve')
+        mirror_product(1, (0, 0, 0))
+        direct_out(1, (0, 0, 1))
+        density(1, 0, 1, 3)
+        overlap_interleave(0, 1, 0, 'act')
+        direct_product(1, (0, 0, 2))
+        density(1, 1, 1, 0)
+        mirror_product(1, (0, 0, 1))
+        overlap_interleave(0, 1, 1, 'dve')
+        density_out(1, 0, 1, 2, 'act')
+        density_out(1, 0, 1, 1, 'dve')
+        multiply(0, (0, 0, 1))
+        density_out(1, 0, 1, 3, 'act')
+        mirror_product(0, (0, 0, 2))
+        multiply(1, (0, 0, 0))
+        density(0, 0, 1, 1)
+        mirror_product(1, (0, 0, 2))
+        direct_out(1, (0, 0, 2))
+        density(1, 1, 1, 1)
+        density_out(1, 1, 1, 0, 'act')
+        quantise(('s', 1, 1))
+        quantise(('s', 0, 1))
+        direct_product(0, (0, 1, 1))
+        multiply(0, (0, 0, 2))
+        direct_product(0, (0, 1, 3))
+        multiply(1, (0, 0, 1))
+        multiply(1, (0, 0, 2))
+        density(1, 1, 1, 3)
+        direct_product(0, (0, 1, 2))
+        density_out(0, 0, 1, 1, 'act')
+        density_out(1, 1, 1, 1, 'act')
+        density_out(1, 1, 1, 3, 'act')
+        direct_out(0, (0, 1, 3))
+        direct_out(0, (0, 1, 1))
+        quantise(('p', 0, 1, 1))
+        direct_product(1, (0, 1, 3))
+        direct_product(1, (0, 1, 1))
+        quantise(('p', 0, 0, 1))
+        mirror_product(0, (0, 1, 3))
+        quantise(('p', 1, 0, 1))
+        direct_product(1, (0, 1, 0))
+        quantise(('p', 1, 1, 1))
+        mirror_product(1, (0, 1, 3))
+        add_channels((0, 0, 1))
+        direct_out(1, (0, 1, 1))
+        multiply(0, (0, 1, 3))
+        direct_product(1, (0, 1, 2))
+        direct_out(0, (0, 1, 2))
+        add_channels((0, 0, 0))
+        mirror_product(0, (0, 1, 2))
+        store_rows(0, 0, 0, 1)
+        direct_out(1, (0, 1, 0))
+        direct_product(0, (1, 1, 2))
+        direct_out(1, (0, 1, 3))
+        direct_product(0, (0, 1, 0))
+        direct_out(0, (0, 1, 0))
+        multiply(1, (0, 1, 3))
+        multiply(0, (0, 1, 2))
+        add_channels((0, 1, 3))
+        mirror_product(1, (0, 1, 0))
+        multiply(1, (0, 1, 0))
+        mirror_product(1, (0, 1, 1))
+        direct_out(1, (0, 1, 2))
+        mirror_product(0, (0, 1, 0))
+        mirror_product(1, (0, 1, 2))
+        multiply(0, (0, 1, 0))
+        mirror_rows(0, 0, 2)
+        multiply(1, (0, 1, 2))
+        direct_out(0, (1, 1, 2))
+        store_rows(0, 0, 1, 1)
+        multiply(1, (0, 1, 1))
+        mirror_rows(0, 0, 3)
+        add_channels((0, 1, 0))
+        mirror_out(0, 0, 2, 'act')
+        add_channels((0, 1, 2))
+        direct_product(0, (1, 1, 0))
+        mirror_product(0, (1, 1, 0))
+        mirror_out(0, 0, 3, 'act')
+        mirror_product(0, (0, 1, 1))
+        direct_out(0, (1, 1, 0))
+        direct_product(1, (1, 1, 2))
+        round_result(0, 0, 0, 'act')
+        direct_product(1, (1, 1, 0))
+        store_rows(0, 1, 2, 1)
+        direct_out(1, (1, 1, 2))
+        direct_product(0, (1, 1, 1))
+        store_rows(0, 1, 3, 1)
+        round_result(0, 0, 1, 'dve')
+        multiply(0, (0, 1, 1))
+        multiply(0, (1, 1, 0))
+        direct_product(1, (1, 1, 1))
+        direct_out(1, (1, 1, 0))
+        add_channels((0, 1, 1))
+        mirror_product(1, (1, 1, 0))
+        quantise_result(0, 0)
+        store_rows(0, 1, 1, 1)
+        multiply(1, (1, 1, 0))
+        direct_out(1, (1, 1, 1))
+        mirror_product(1, (1, 1, 2))
+        mirror_product(1, (1, 1, 1))
+        mirror_product(0, (1, 1, 1))
+        store_rows(0, 0, 2, 1)
+        add_channels((1, 1, 0))
+        multiply(1, (1, 1, 1))
+        mirror_product(0, (1, 1, 2))
+        direct_out(0, (1, 1, 1))
+        mirror_rows(1, 0, 1)
+        round_result(0, 1, 1, 'act')
+        round_result(0, 1, 0, 'act')
+        mirror_out(1, 0, 1, 'act')
+        multiply(1, (1, 1, 2))
+        store_rows(0, 0, 3, 1)
+        mirror_rows(1, 0, 0)
+        mirror_out(1, 0, 0, 'act')
+        multiply(0, (1, 1, 1))
+        mirror_rows(1, 0, 2)
+        multiply(0, (1, 1, 2))
+        store_rows(0, 1, 0, 1)
+        add_channels((1, 1, 1))
+        store_rows(1, 1, 0, 1)
+        mirror_rows(1, 0, 3)
+        store_words(0, 0)
+        store_rows(1, 0, 1, 1)
+        mirror_out(1, 0, 2, 'act')
+        store_rows(1, 0, 0, 1)
+        store_rows(1, 1, 1, 1)
+        mirror_out(1, 0, 3, 'act')
+        quantise_result(0, 1)
+        store_words(0, 1)
+        store_scales(0)
+        mirror_rows(1, 1, 2)
+        store_rows(1, 0, 2, 1)
+        round_result(1, 0, 0, 'dve')
+        store_rows(1, 0, 3, 1)
+        mirror_rows(1, 1, 3)
+        mirror_out(1, 1, 2, 'act')
+        store_rows(1, 1, 2, 1)
+        mirror_out(1, 1, 3, 'act')
+        round_result(1, 0, 1, 'dve')
+        round_result(1, 1, 0, 'act')
+        round_result(1, 1, 1, 'dve')
+        quantise_result(1, 0)
+        store_rows(1, 1, 3, 1)
+        quantise_result(1, 1)
+        store_words(1, 0)
+        store_words(1, 1)
+        store_scales(1)

@@ -29,7 +29,7 @@ def tile_biorthogonalspinmayerbondorder_x1_kernel(tc, l, r, occ, s, out_0, out_1
         psum = ctx.enter_context(tc.psum_pool(name="psum", bufs=8))
         ctx.enter_context(tc.manual_schedule())
 
-        raw, staged, quantised, banks, products, result = {}, {}, {}, {}, {}, {}
+        raw, staged, quantised, banks, products, result, summed = {}, {}, {}, {}, {}, {}, {}
 
         def bank(key):
             banks[key] = psum.tile([P, GROUP], F32, name="bank")
@@ -115,37 +115,41 @@ def tile_biorthogonalspinmayerbondorder_x1_kernel(tc, l, r, occ, s, out_0, out_1
 
         def overlap_interleave(h, g, half, engine):
             c = slice(2 * half, 2 * half + 2)
-            copier(engine)(
-                out=stage(("s", h, g))[:].rearrange("p (c q j) -> p c q j", c=PACK, j=PACK)[:, c],
-                in_=raw["s", h, g][:].rearrange("p j (q c) -> p c q j", c=PACK)[:, c],
-            )
+            dst = stage(("s", h, g))[:].rearrange("p (c q j) -> p c q j", c=PACK, j=PACK)[:, c]
+            src = raw["s", h, g][:].rearrange("p j (q c) -> p c q j", c=PACK)[:, c]
+            if engine == "pool":
+                nc.gpsimd.tensor_scalar(out=dst, in0=src, scalar1=1.0, scalar2=0.0, op0=MULT, op1=ADD)
+            else:
+                copier(engine)(out=dst, in_=src)
 
-        def pieces_of(unit):
+        def pieces_of(t, unit):
             g, g2, j = unit
-            if g == g2 and j == 2:
-                return [(2, block(0, 2), block(2, 2)), (3, block(2, 2), block(2, 2))]
-            return [(j, block(0, 4), block(0, 4))]
+            if g != g2 or j == 0:
+                return [(t, j, block(0, 4), block(0, 4))]
+            if j == 1:
+                return [(t, 1, block(0, 2), block(1, 2)), (t, 1, block(2), block(3)), (t, 3, block(3), block(3))]
+            return [(t2, 2, block(2 * t2, 2), block(2, 2)) for t2 in range(T)]
 
         def direct_product(t, unit):
             g, g2, _ = unit
             direct = bank(("x", t, unit))
-            for j, at, cols in pieces_of(unit):
+            for t2, j, at, cols in pieces_of(t, unit):
                 for h in range(G):
-                    mx(direct[:, at], ("p", t, h, g), block(j), ("s", h, g2), cols, h == 0, h == G - 1)
+                    mx(direct[:, at], ("p", t2, h, g), block(j), ("s", h, g2), cols, h == 0, h == G - 1)
 
         def mirror_product(t, unit):
             g, g2, _ = unit
             mirror = bank(("y", t, unit))
-            for j, at, cols in pieces_of(unit):
+            for t2, j, at, cols in pieces_of(t, unit):
                 for h in range(G):
-                    mx(mirror[:, at], ("s", h, g), block(j), ("p", t, h, g2), cols, h == 0, h == G - 1)
+                    mx(mirror[:, at], ("s", h, g), block(j), ("p", t2, h, g2), cols, h == 0, h == G - 1)
 
         def direct_out(t, unit):
             staged["x", t, unit] = work.tile([P, GROUP], F32, name="direct", bufs=6)
             nc.scalar.copy(out=staged["x", t, unit][:], in_=banks["x", t, unit][:])
 
         def multiply(t, unit):
-            products[t, unit] = keep.tile([P, GROUP], F32, name="product_%d_%d%d%d" % ((t,) + unit))
+            products[t, unit] = work.tile([P, GROUP], F32, name="product", bufs=10)
             nc.vector.scalar_tensor_tensor(
                 out=products[t, unit][:], in0=banks["y", t, unit][:], scalar=2.0, in1=staged["x", t, unit][:], op0=MULT, op1=MULT
             )
@@ -155,29 +159,47 @@ def tile_biorthogonalspinmayerbondorder_x1_kernel(tc, l, r, occ, s, out_0, out_1
                 result[g, g2] = keep.tile([P, PACK, GROUP], F32, name="result_%d%d" % (g, g2))
             return result[g, g2]
 
-        def add_channels(unit, engine="dve"):
+        def sums(g, g2):
+            if (g, g2) not in summed:
+                summed[g, g2] = keep.tile([P, (13 if g == g2 else 16) * P], F32, name="sums_%d%d" % (g, g2))
+            return summed[g, g2]
+
+        def place(g, g2, j, c):
+            if g != g2:
+                return PACK * j + c
+            return {0: 0, 1: 4, 2: 9, 3: 5}[j] + c
+
+        def add_channels(unit, engine):
             g, g2, j = unit
-            (nc.vector if engine == "dve" else nc.gpsimd).tensor_tensor(
-                out=quadrant(g, g2)[:, j, :].rearrange("p (q c) -> p q c", c=PACK),
-                in0=products[0, unit][:].rearrange("p (c q) -> p q c", c=PACK),
-                in1=products[1, unit][:].rearrange("p (c q) -> p q c", c=PACK),
-                op=ADD,
-            )
+            if g == g2 and j == 2:
+                dst = block(place(g, g, 2, 2), 2)
+                first, second = products[0, unit][:, block(0, 2)], products[0, unit][:, block(2, 2)]
+            else:
+                dst = block(place(g, g2, j, j if g == g2 else 0), 4)
+                first, second = products[0, unit][:], products[1, unit][:]
+            (nc.vector if engine == "dve" else nc.gpsimd).tensor_tensor(out=sums(g, g2)[:, dst], in0=first, in1=second, op=ADD)
 
         def mirror_rows(g, g2, j):
             dst = bank(("m", g, g2, j))
-            for c in range(PACK):
-                for t in range(T):
-                    if g == g2 and c >= 2:
-                        src = products[t, (g, g, 2)][:, block(2 * (c - 2) + j - 2)]
-                    else:
-                        src = products[t, (g2, g, c)][:, block(j)]
-                    nc.tensor.matmul(out=dst[:, block(c)], lhsT=src, rhs=ident[:], start=t == 0, stop=t == T - 1, is_transpose=True)
+            wanted = [(1, 0), (2, 0), (2, 1)] if (g == g2 and j == 1) else [(j, c) for c in range(PACK)]
+            for at, (row, c) in enumerate(wanted):
+                nc.tensor.transpose(dst[:, block(at)], sums(g2, g)[:, block(place(g2, g, c, row))], ident[:])
 
-        def mirror_out(g, g2, j, engine="act"):
+        def mirror_out(g, g2, j, engine):
+            src = banks["m", g, g2, j]
+            if g == g2 and j == 1:
+                copier(engine)(out=sums(g, g)[:, block(place(g, g, 1, 0))], in_=src[:, block(0)])
+                copier(engine)(out=sums(g, g)[:, block(place(g, g, 2, 0), 2)], in_=src[:, block(1, 2)])
+            else:
+                copier(engine)(
+                    out=quadrant(g, g2)[:, j, :].rearrange("p (q c) -> p q c", c=PACK),
+                    in_=src[:].rearrange("p (c q) -> p q c", c=PACK),
+                )
+
+        def order_row(g, g2, j, engine):
             copier(engine)(
                 out=quadrant(g, g2)[:, j, :].rearrange("p (q c) -> p q c", c=PACK),
-                in_=banks["m", g, g2, j][:].rearrange("p (c q) -> p q c", c=PACK),
+                in_=sums(g, g2)[:, block(place(g, g2, j, 0), 4)].rearrange("p (c q) -> p q c", c=PACK),
             )
 
         def store_rows(g, g2, j0, count):
@@ -213,278 +235,282 @@ def tile_biorthogonalspinmayerbondorder_x1_kernel(tc, l, r, occ, s, out_0, out_1
         nc.scalar.dma_start(out=occ_sb[:], in_=occ.rearrange("t (p j) -> p t j", j=PACK))
         out_scales = [keep.tile([P, N], U8, name="out_scales_%d" % g, align_bytes=64) for g in range(G)]
 
-        load_orbitals('l', 0, 0, 0, 2)
         load_orbitals('l', 0, 0, 2, 2)
+        load_orbitals('l', 0, 0, 0, 2)
         turn('l', 0, 0, 0)
-        turn('l', 0, 0, 1)
-        load_orbitals('r', 0, 0, 2, 2)
-        load_orbitals('r', 0, 0, 0, 2)
-        turn('r', 0, 0, 1)
-        turn_out('r', 0, 0, 1, 'act')
-        turn('r', 0, 0, 0)
         load_orbitals('r', 0, 1, 0, 4)
-        turn_out('l', 0, 0, 0, 'act')
-        turn('r', 0, 1, 0)
-        turn_out('r', 0, 1, 0, 'act')
-        load_orbitals('r', 1, 0, 0, 4)
-        load_overlap(0, 0)
+        turn('l', 0, 0, 1)
         turn('r', 0, 1, 1)
-        turn_out('l', 0, 0, 1, 'act')
-        turn_out('r', 0, 0, 0, 'dve')
-        turn_out('r', 0, 1, 1, 'act')
-        quantise(('l', 0, 0))
-        quantise(('r', 0, 0))
-        overlap_interleave(0, 0, 1, 'act')
-        turn('r', 1, 0, 0)
-        density(0, 0, 0, 3)
-        load_orbitals('l', 1, 0, 0, 4)
-        density(0, 0, 0, 1)
-        turn('r', 1, 0, 1)
         load_orbitals('r', 1, 1, 0, 4)
-        load_overlap(1, 0)
-        turn('l', 1, 0, 1)
-        turn('l', 1, 0, 0)
-        overlap_interleave(0, 0, 0, 'act')
-        turn_out('r', 1, 0, 1, 'act')
-        turn_out('r', 1, 0, 0, 'dve')
-        load_orbitals('l', 0, 1, 0, 4)
-        turn('r', 1, 1, 1)
-        quantise(('r', 0, 1))
-        density_out(0, 0, 0, 1, 'dve')
+        load_orbitals('l', 1, 0, 0, 4)
+        turn_out('r', 0, 1, 1, 'act')
+        turn_out('l', 0, 0, 1, 'dve')
+        turn_out('l', 0, 0, 0, 'dve')
+        turn('r', 0, 1, 0)
         turn('r', 1, 1, 0)
-        density(0, 1, 0, 0)
-        density_out(0, 0, 0, 3, 'dve')
-        turn_out('l', 1, 0, 1, 'act')
-        density(0, 1, 0, 2)
+        quantise(('l', 0, 0))
+        turn('r', 1, 1, 1)
+        turn('l', 1, 0, 1)
+        turn_out('r', 0, 1, 0, 'act')
+        load_overlap(1, 0)
+        quantise(('r', 0, 1))
+        turn_out('r', 1, 1, 0, 'act')
         turn_out('r', 1, 1, 1, 'act')
-        density(0, 0, 0, 2)
-        turn_out('l', 1, 0, 0, 'act')
-        turn('l', 0, 1, 0)
-        turn('l', 0, 1, 1)
+        turn_out('l', 1, 0, 1, 'dve')
         overlap_interleave(1, 0, 0, 'act')
-        overlap_interleave(1, 0, 1, 'dve')
-        density(0, 0, 0, 0)
-        density_out(0, 1, 0, 0, 'act')
-        density_out(0, 0, 0, 2, 'act')
-        quantise(('r', 1, 0))
-        density(0, 1, 0, 3)
-        density_out(0, 1, 0, 2, 'act')
-        turn_out('r', 1, 1, 0, 'dve')
-        density_out(0, 1, 0, 3, 'act')
-        quantise(('l', 1, 0))
-        density(1, 0, 0, 0)
-        density(1, 0, 0, 2)
-        quantise(('r', 1, 1))
+        turn('l', 1, 0, 0)
         load_orbitals('l', 1, 1, 0, 4)
+        density(0, 1, 0, 0)
+        density(0, 1, 0, 2)
+        overlap_interleave(1, 0, 1, 'dve')
         density(0, 1, 0, 1)
-        density_out(0, 0, 0, 0, 'act')
-        load_overlap(1, 1)
-        density(1, 1, 0, 3)
-        turn_out('l', 0, 1, 0, 'act')
-        density_out(1, 0, 0, 0, 'act')
-        density(1, 0, 0, 3)
-        turn_out('l', 0, 1, 1, 'act')
-        density_out(1, 0, 0, 3, 'act')
-        density(1, 0, 0, 1)
+        turn_out('l', 1, 0, 0, 'dve')
+        density_out(0, 1, 0, 2, 'act')
+        load_orbitals('r', 1, 0, 0, 4)
+        density(0, 1, 0, 3)
         turn('l', 1, 1, 0)
-        density(1, 1, 0, 2)
-        density_out(1, 0, 0, 2, 'dve')
-        quantise(('l', 0, 1))
-        density_out(0, 1, 0, 1, 'act')
-        density(0, 0, 1, 0)
-        quantise(('s', 1, 0))
         turn('l', 1, 1, 1)
-        density_out(1, 1, 0, 3, 'act')
-        density(0, 0, 1, 2)
-        density_out(1, 0, 0, 1, 'act')
-        quantise(('p', 0, 0, 0))
-        density(1, 1, 0, 0)
-        density_out(1, 1, 0, 2, 'act')
-        turn_out('l', 1, 1, 0, 'act')
-        quantise(('p', 0, 1, 0))
-        density(0, 1, 1, 1)
-        quantise(('s', 0, 0))
+        quantise(('r', 1, 1))
+        turn('r', 1, 0, 0)
+        density_out(0, 1, 0, 0, 'act')
+        density_out(0, 1, 0, 1, 'act')
+        load_overlap(0, 0)
+        turn('r', 1, 0, 1)
+        quantise(('l', 1, 0))
+        turn_out('l', 1, 1, 0, 'dve')
+        density_out(0, 1, 0, 3, 'act')
+        overlap_interleave(0, 0, 1, 'dve')
+        load_orbitals('r', 0, 0, 0, 2)
         density(1, 1, 0, 1)
-        turn_out('l', 1, 1, 1, 'act')
-        density_out(0, 0, 1, 0, 'act')
-        density_out(1, 1, 0, 1, 'dve')
-        density_out(0, 0, 1, 2, 'act')
-        density(0, 1, 1, 0)
-        density_out(1, 1, 0, 0, 'act')
-        density(0, 0, 1, 3)
-        density_out(0, 0, 1, 3, 'dve')
-        quantise(('p', 1, 1, 0))
-        direct_product(0, (0, 0, 0))
-        density_out(0, 1, 1, 1, 'act')
-        density_out(0, 1, 1, 0, 'act')
-        density(0, 1, 1, 3)
-        direct_product(0, (0, 0, 1))
-        direct_product(0, (0, 0, 2))
-        direct_out(0, (0, 0, 0))
-        load_overlap(0, 1)
-        mirror_product(0, (0, 0, 0))
-        density_out(0, 1, 1, 3, 'act')
+        overlap_interleave(0, 0, 0, 'act')
+        density(1, 1, 0, 0)
+        load_orbitals('l', 0, 1, 0, 4)
+        turn_out('l', 1, 1, 1, 'dve')
+        turn_out('r', 1, 0, 1, 'act')
+        quantise(('s', 1, 0))
+        load_orbitals('r', 0, 0, 2, 2)
+        turn_out('r', 1, 0, 0, 'act')
+        density_out(1, 1, 0, 1, 'act')
+        turn('r', 0, 0, 0)
+        density_out(1, 1, 0, 0, 'dve')
         quantise(('l', 1, 1))
-        density(0, 1, 1, 2)
-        density(1, 0, 1, 0)
-        density(1, 1, 1, 2)
-        quantise(('p', 1, 0, 0))
-        direct_product(1, (0, 0, 1))
-        direct_out(0, (0, 0, 1))
-        overlap_interleave(1, 1, 0, 'dve')
-        direct_product(1, (0, 0, 0))
-        direct_out(0, (0, 0, 2))
-        density_out(1, 0, 1, 0, 'act')
-        mirror_product(0, (0, 0, 1))
-        density(1, 0, 1, 1)
-        density_out(1, 1, 1, 2, 'act')
-        multiply(0, (0, 0, 0))
-        direct_out(1, (0, 0, 0))
-        density(1, 0, 1, 2)
-        density_out(0, 1, 1, 2, 'dve')
-        overlap_interleave(1, 1, 1, 'dve')
-        mirror_product(1, (0, 0, 0))
-        direct_out(1, (0, 0, 1))
-        density(1, 0, 1, 3)
-        overlap_interleave(0, 1, 0, 'act')
-        direct_product(1, (0, 0, 2))
+        turn('r', 0, 0, 1)
+        turn('l', 0, 1, 1)
+        turn_out('r', 0, 0, 0, 'act')
+        quantise(('r', 1, 0))
+        turn('l', 0, 1, 0)
         density(1, 1, 1, 0)
+        density(1, 1, 0, 2)
+        density(1, 0, 0, 2)
+        turn_out('l', 0, 1, 1, 'dve')
+        turn_out('r', 0, 0, 1, 'act')
+        turn_out('l', 0, 1, 0, 'dve')
+        density(1, 1, 0, 3)
+        density_out(1, 1, 1, 0, 'act')
+        density_out(1, 1, 0, 2, 'act')
+        quantise(('r', 0, 0))
+        quantise(('l', 0, 1))
+        density_out(1, 1, 0, 3, 'act')
+        density(1, 0, 0, 0)
+        density_out(1, 0, 0, 2, 'dve')
+        density(1, 0, 0, 1)
+        density(1, 0, 0, 3)
+        density(1, 0, 1, 1)
+        density_out(1, 0, 0, 0, 'act')
+        density_out(1, 0, 0, 1, 'act')
+        density_out(1, 0, 1, 1, 'act')
+        density_out(1, 0, 0, 3, 'dve')
+        quantise(('s', 0, 0))
+        density(0, 0, 1, 2)
+        load_overlap(1, 1)
+        density(0, 0, 0, 0)
+        quantise(('p', 1, 0, 0))
+        density(0, 0, 0, 1)
+        density(1, 0, 1, 3)
+        density(1, 1, 1, 3)
+        density_out(0, 0, 1, 2, 'act')
+        quantise(('p', 1, 1, 0))
+        density_out(0, 0, 0, 0, 'act')
+        density(0, 0, 0, 3)
+        load_overlap(0, 1)
+        density(1, 1, 1, 2)
+        density(0, 0, 0, 2)
+        density_out(0, 0, 0, 1, 'act')
+        density(0, 1, 1, 3)
+        density_out(1, 1, 1, 3, 'dve')
+        density_out(1, 0, 1, 3, 'act')
+        density_out(0, 0, 0, 2, 'dve')
+        direct_product(1, (0, 0, 0))
+        direct_product(1, (0, 0, 1))
+        density(1, 0, 1, 2)
+        overlap_interleave(1, 1, 0, 'dve')
+        density_out(0, 0, 0, 3, 'act')
+        density(0, 0, 1, 0)
+        quantise(('p', 0, 1, 0))
         mirror_product(1, (0, 0, 1))
+        density_out(1, 1, 1, 2, 'act')
+        quantise(('p', 0, 0, 0))
+        density(1, 0, 1, 0)
+        density_out(0, 1, 1, 3, 'act')
+        density(1, 1, 1, 1)
+        overlap_interleave(0, 1, 0, 'dve')
+        direct_out(1, (0, 0, 0))
+        direct_out(1, (0, 0, 1))
         overlap_interleave(0, 1, 1, 'dve')
         density_out(1, 0, 1, 2, 'act')
-        density_out(1, 0, 1, 1, 'dve')
-        multiply(0, (0, 0, 1))
-        density_out(1, 0, 1, 3, 'act')
-        mirror_product(0, (0, 0, 2))
-        multiply(1, (0, 0, 0))
-        density(0, 0, 1, 1)
-        mirror_product(1, (0, 0, 2))
-        direct_out(1, (0, 0, 2))
-        density(1, 1, 1, 1)
-        density_out(1, 1, 1, 0, 'act')
-        quantise(('s', 1, 1))
-        quantise(('s', 0, 1))
-        direct_product(0, (0, 1, 1))
-        multiply(0, (0, 0, 2))
-        direct_product(0, (0, 1, 3))
+        density_out(0, 0, 1, 0, 'act')
         multiply(1, (0, 0, 1))
-        multiply(1, (0, 0, 2))
-        density(1, 1, 1, 3)
-        direct_product(0, (0, 1, 2))
-        density_out(0, 0, 1, 1, 'act')
+        density_out(1, 0, 1, 0, 'act')
+        direct_product(0, (0, 0, 0))
         density_out(1, 1, 1, 1, 'act')
-        density_out(1, 1, 1, 3, 'act')
-        direct_out(0, (0, 1, 3))
-        direct_out(0, (0, 1, 1))
-        quantise(('p', 0, 1, 1))
-        direct_product(1, (0, 1, 3))
-        direct_product(1, (0, 1, 1))
-        quantise(('p', 0, 0, 1))
-        mirror_product(0, (0, 1, 3))
-        quantise(('p', 1, 0, 1))
-        direct_product(1, (0, 1, 0))
+        direct_product(0, (0, 0, 1))
+        overlap_interleave(1, 1, 1, 'dve')
+        quantise(('s', 0, 1))
+        mirror_product(1, (0, 0, 0))
+        density(0, 1, 1, 0)
+        quantise(('s', 1, 1))
+        direct_product(0, (0, 0, 2))
+        mirror_product(0, (0, 0, 1))
+        direct_out(0, (0, 0, 1))
+        direct_out(0, (0, 0, 0))
+        mirror_product(0, (0, 0, 2))
+        density(0, 0, 1, 3)
         quantise(('p', 1, 1, 1))
-        mirror_product(1, (0, 1, 3))
-        add_channels((0, 0, 1))
-        direct_out(1, (0, 1, 1))
-        multiply(0, (0, 1, 3))
-        direct_product(1, (0, 1, 2))
+        multiply(1, (0, 0, 0))
+        direct_product(0, (0, 1, 2))
+        direct_out(0, (0, 0, 2))
+        density(0, 1, 1, 2)
+        mirror_product(0, (0, 0, 0))
+        density_out(0, 1, 1, 0, 'act')
         direct_out(0, (0, 1, 2))
-        add_channels((0, 0, 0))
-        mirror_product(0, (0, 1, 2))
-        store_rows(0, 0, 0, 1)
+        density(0, 0, 1, 1)
+        density_out(0, 1, 1, 2, 'act')
+        multiply(0, (0, 0, 1))
+        multiply(0, (0, 0, 2))
+        quantise(('p', 1, 0, 1))
+        multiply(0, (0, 0, 0))
+        add_channels((0, 0, 1), 'dve')
+        density_out(0, 0, 1, 3, 'act')
+        density_out(0, 0, 1, 1, 'act')
+        direct_product(1, (0, 1, 0))
+        density(0, 1, 1, 1)
+        direct_product(0, (0, 1, 3))
+        add_channels((0, 0, 0), 'dve')
+        add_channels((0, 0, 2), 'dve')
+        quantise(('p', 0, 0, 1))
         direct_out(1, (0, 1, 0))
-        direct_product(0, (1, 1, 2))
-        direct_out(1, (0, 1, 3))
-        direct_product(0, (0, 1, 0))
-        direct_out(0, (0, 1, 0))
-        multiply(1, (0, 1, 3))
-        multiply(0, (0, 1, 2))
-        add_channels((0, 1, 3))
-        mirror_product(1, (0, 1, 0))
-        multiply(1, (0, 1, 0))
-        mirror_product(1, (0, 1, 1))
-        direct_out(1, (0, 1, 2))
-        mirror_product(0, (0, 1, 0))
-        mirror_product(1, (0, 1, 2))
-        multiply(0, (0, 1, 0))
-        mirror_rows(0, 0, 2)
-        multiply(1, (0, 1, 2))
-        direct_out(0, (1, 1, 2))
-        store_rows(0, 0, 1, 1)
-        multiply(1, (0, 1, 1))
+        direct_product(1, (0, 1, 3))
+        direct_product(1, (0, 1, 2))
+        density_out(0, 1, 1, 1, 'act')
+        quantise(('p', 0, 1, 1))
+        mirror_rows(0, 0, 1)
+        mirror_out(0, 0, 1, 'dve')
         mirror_rows(0, 0, 3)
-        add_channels((0, 1, 0))
-        mirror_out(0, 0, 2, 'act')
-        add_channels((0, 1, 2))
-        direct_product(0, (1, 1, 0))
-        mirror_product(0, (1, 1, 0))
-        mirror_out(0, 0, 3, 'act')
-        mirror_product(0, (0, 1, 1))
-        direct_out(0, (1, 1, 0))
-        direct_product(1, (1, 1, 2))
+        direct_out(1, (0, 1, 3))
+        mirror_out(0, 0, 3, 'dve')
+        direct_out(1, (0, 1, 2))
+        order_row(0, 0, 0, 'act')
+        mirror_product(1, (0, 1, 0))
+        mirror_product(1, (0, 1, 2))
+        direct_product(0, (0, 1, 0))
+        direct_out(0, (0, 1, 3))
+        order_row(0, 0, 2, 'dve')
+        order_row(0, 0, 1, 'act')
+        mirror_product(0, (0, 1, 2))
+        multiply(1, (0, 1, 2))
+        mirror_product(1, (0, 1, 3))
+        direct_out(0, (0, 1, 0))
+        multiply(1, (0, 1, 0))
+        mirror_product(0, (0, 1, 3))
+        mirror_product(0, (0, 1, 0))
         round_result(0, 0, 0, 'act')
-        direct_product(1, (1, 1, 0))
-        store_rows(0, 1, 2, 1)
-        direct_out(1, (1, 1, 2))
-        direct_product(0, (1, 1, 1))
-        store_rows(0, 1, 3, 1)
-        round_result(0, 0, 1, 'dve')
+        multiply(0, (0, 1, 2))
+        multiply(1, (0, 1, 3))
+        multiply(0, (0, 1, 3))
+        direct_product(0, (0, 1, 1))
+        round_result(0, 0, 1, 'act')
+        multiply(0, (0, 1, 0))
+        direct_out(0, (0, 1, 1))
+        direct_product(1, (0, 1, 1))
+        add_channels((0, 1, 3), 'dve')
+        mirror_product(0, (0, 1, 1))
+        add_channels((0, 1, 2), 'dve')
+        direct_out(1, (0, 1, 1))
+        mirror_product(1, (0, 1, 1))
         multiply(0, (0, 1, 1))
-        multiply(0, (1, 1, 0))
+        store_rows(0, 0, 0, 1)
+        direct_product(0, (1, 1, 1))
+        direct_product(1, (1, 1, 0))
+        multiply(1, (0, 1, 1))
+        add_channels((0, 1, 0), 'dve')
+        add_channels((0, 1, 1), 'dve')
+        order_row(0, 1, 3, 'act')
+        store_rows(0, 1, 3, 1)
+        direct_product(0, (1, 1, 0))
+        order_row(0, 1, 0, 'dve')
+        mirror_product(0, (1, 1, 0))
         direct_product(1, (1, 1, 1))
-        direct_out(1, (1, 1, 0))
-        add_channels((0, 1, 1))
-        mirror_product(1, (1, 1, 0))
-        quantise_result(0, 0)
-        store_rows(0, 1, 1, 1)
-        multiply(1, (1, 1, 0))
-        direct_out(1, (1, 1, 1))
-        mirror_product(1, (1, 1, 2))
-        mirror_product(1, (1, 1, 1))
-        mirror_product(0, (1, 1, 1))
-        store_rows(0, 0, 2, 1)
-        add_channels((1, 1, 0))
-        multiply(1, (1, 1, 1))
-        mirror_product(0, (1, 1, 2))
         direct_out(0, (1, 1, 1))
-        mirror_rows(1, 0, 1)
-        round_result(0, 1, 1, 'act')
-        round_result(0, 1, 0, 'act')
-        mirror_out(1, 0, 1, 'act')
-        multiply(1, (1, 1, 2))
-        store_rows(0, 0, 3, 1)
-        mirror_rows(1, 0, 0)
-        mirror_out(1, 0, 0, 'act')
+        mirror_product(0, (1, 1, 1))
+        direct_out(1, (1, 1, 0))
+        direct_out(0, (1, 1, 0))
+        mirror_product(1, (1, 1, 1))
+        store_rows(0, 0, 1, 1)
+        order_row(0, 1, 2, 'dve')
+        order_row(0, 1, 1, 'act')
+        quantise_result(0, 0)
+        mirror_product(1, (1, 1, 0))
+        direct_out(1, (1, 1, 1))
+        multiply(0, (1, 1, 0))
         multiply(0, (1, 1, 1))
+        mirror_product(0, (1, 1, 2))
+        direct_product(0, (1, 1, 2))
+        mirror_rows(1, 0, 1)
         mirror_rows(1, 0, 2)
-        multiply(0, (1, 1, 2))
-        store_rows(0, 1, 0, 1)
-        add_channels((1, 1, 1))
-        store_rows(1, 1, 0, 1)
-        mirror_rows(1, 0, 3)
+        multiply(1, (1, 1, 1))
+        round_result(0, 1, 0, 'act')
+        multiply(1, (1, 1, 0))
+        store_rows(0, 0, 3, 1)
+        round_result(0, 1, 1, 'act')
+        add_channels((1, 1, 1), 'dve')
         store_words(0, 0)
-        store_rows(1, 0, 1, 1)
-        mirror_out(1, 0, 2, 'act')
-        store_rows(1, 0, 0, 1)
-        store_rows(1, 1, 1, 1)
-        mirror_out(1, 0, 3, 'act')
+        add_channels((1, 1, 0), 'dve')
+        mirror_rows(1, 0, 0)
+        store_rows(0, 1, 2, 1)
+        mirror_rows(1, 1, 1)
+        store_rows(0, 0, 2, 1)
+        direct_out(0, (1, 1, 2))
+        mirror_out(1, 0, 1, 'act')
+        store_rows(0, 1, 1, 1)
         quantise_result(0, 1)
+        store_rows(0, 1, 0, 1)
         store_words(0, 1)
-        store_scales(0)
-        mirror_rows(1, 1, 2)
-        store_rows(1, 0, 2, 1)
-        round_result(1, 0, 0, 'dve')
-        store_rows(1, 0, 3, 1)
+        mirror_rows(1, 0, 3)
+        mirror_out(1, 0, 0, 'act')
+        multiply(0, (1, 1, 2))
+        mirror_out(1, 0, 2, 'dve')
+        store_rows(1, 0, 1, 1)
+        add_channels((1, 1, 2), 'dve')
+        mirror_out(1, 1, 1, 'act')
+        store_rows(1, 0, 0, 1)
+        order_row(1, 1, 0, 'dve')
+        mirror_out(1, 0, 3, 'act')
+        order_row(1, 1, 1, 'act')
         mirror_rows(1, 1, 3)
-        mirror_out(1, 1, 2, 'act')
-        store_rows(1, 1, 2, 1)
-        mirror_out(1, 1, 3, 'act')
+        store_rows(1, 0, 2, 1)
+        store_scales(0)
+        order_row(1, 1, 2, 'dve')
+        store_rows(1, 0, 3, 1)
         round_result(1, 0, 1, 'dve')
-        round_result(1, 1, 0, 'act')
-        round_result(1, 1, 1, 'dve')
-        quantise_result(1, 0)
+        round_result(1, 0, 0, 'dve')
+        store_rows(1, 1, 0, 1)
+        store_rows(1, 1, 1, 1)
+        mirror_out(1, 1, 3, 'act')
+        store_rows(1, 1, 2, 1)
+        round_result(1, 1, 0, 'dve')
+        round_result(1, 1, 1, 'act')
         store_rows(1, 1, 3, 1)
+        quantise_result(1, 0)
         quantise_result(1, 1)
         store_words(1, 0)
         store_words(1, 1)

@@ -46,10 +46,9 @@ def tile_biorthogonalspinmayerbondorder_x1_kernel(tc, l, r, occ, s, out_0, out_1
                 raw[which, t, g, j0 + j] = piece[:, j, :]
 
         def load_overlap(h, g):
-            piece = keep.tile([P, PACK, GROUP], BF16, name="raw_s%d%d" % (h, g))
-            src = s[h * GROUP : (h + 1) * GROUP, g * GROUP : (g + 1) * GROUP]
-            nc.sync.dma_start(out=piece[:], in_=src.rearrange("(p j) d -> p j d", j=PACK))
-            raw["s", h, g] = piece
+            piece = keep.tile([P, PACK, N], BF16, name="raw_s%d" % h)
+            nc.sync.dma_start(out=piece[:], in_=s[h * GROUP : (h + 1) * GROUP, :].rearrange("(p j) d -> p j d", j=PACK))
+            raw["s", h] = piece
 
         def stage(key):
             if key not in staged:
@@ -114,9 +113,9 @@ def tile_biorthogonalspinmayerbondorder_x1_kernel(tc, l, r, occ, s, out_0, out_1
             )
 
         def overlap_interleave(h, g, half, engine):
-            c = slice(2 * half, 2 * half + 2)
-            dst = stage(("s", h, g))[:].rearrange("p (c q j) -> p c q j", c=PACK, j=PACK)[:, c]
-            src = raw["s", h, g][:].rearrange("p j (q c) -> p c q j", c=PACK)[:, c]
+            pairs = slice(half * P // 4, (half + 1) * P // 4)
+            dst = stage(("s", h, g))[:].rearrange("p (c q e j) -> p q c e j", c=PACK, e=2, j=PACK)[:, pairs]
+            src = raw["s", h][:, :, g * GROUP : (g + 1) * GROUP].rearrange("p j (q e c) -> p q c e j", e=2, c=PACK)[:, pairs]
             if engine == "pool":
                 nc.gpsimd.tensor_scalar(out=dst, in0=src, scalar1=1.0, scalar2=0.0, op0=MULT, op1=ADD)
             else:
@@ -213,11 +212,14 @@ def tile_biorthogonalspinmayerbondorder_x1_kernel(tc, l, r, occ, s, out_0, out_1
                 in_=result[g, g2][:].rearrange("p j m -> p m j")[:, m, :],
             )
 
-        def quantise_result(g, g2):
-            cols = slice(g2 * GROUP, (g2 + 1) * GROUP)
-            codes = keep.tile([P, GROUP], U32, name="out_codes_%d%d" % (g, g2), align_bytes=64)
-            nc.vector.quantize_mx(out=codes[:].bitcast(FP8X4), scales=out_scales[g][:, cols], in_=staged["o", g, g2][:])
-            quantised["o", g, g2] = codes
+        def quantise_result(g, g2, half):
+            if ("o", g, g2) not in quantised:
+                quantised["o", g, g2] = keep.tile([P, GROUP], U32, name="out_codes_%d%d" % (g, g2), align_bytes=64)
+            nc.vector.quantize_mx(
+                out=quantised["o", g, g2][:, block(2 * half, 2)].bitcast(FP8X4),
+                scales=out_scales[g][:, block(PACK * g2 + 2 * half, 2)],
+                in_=staged["o", g, g2][:, half * 2 * GROUP : (half + 1) * 2 * GROUP],
+            )
 
         def store_words(g, g2):
             words = out_1[g].rearrange("p m j -> p (m j)").bitcast(I32)
@@ -235,283 +237,285 @@ def tile_biorthogonalspinmayerbondorder_x1_kernel(tc, l, r, occ, s, out_0, out_1
         nc.scalar.dma_start(out=occ_sb[:], in_=occ.rearrange("t (p j) -> p t j", j=PACK))
         out_scales = [keep.tile([P, N], U8, name="out_scales_%d" % g, align_bytes=64) for g in range(G)]
 
-        load_orbitals('l', 0, 0, 2, 2)
-        load_orbitals('l', 0, 0, 0, 2)
-        turn('l', 0, 0, 0)
-        load_orbitals('r', 0, 1, 0, 4)
-        turn('l', 0, 0, 1)
-        turn('r', 0, 1, 1)
-        load_orbitals('r', 1, 1, 0, 4)
-        load_orbitals('l', 1, 0, 0, 4)
-        turn_out('r', 0, 1, 1, 'act')
-        turn_out('l', 0, 0, 1, 'dve')
-        turn_out('l', 0, 0, 0, 'dve')
-        turn('r', 0, 1, 0)
-        turn('r', 1, 1, 0)
-        quantise(('l', 0, 0))
-        turn('r', 1, 1, 1)
-        turn('l', 1, 0, 1)
-        turn_out('r', 0, 1, 0, 'act')
-        load_overlap(1, 0)
-        quantise(('r', 0, 1))
-        turn_out('r', 1, 1, 0, 'act')
-        turn_out('r', 1, 1, 1, 'act')
-        turn_out('l', 1, 0, 1, 'dve')
-        overlap_interleave(1, 0, 0, 'act')
-        turn('l', 1, 0, 0)
-        load_orbitals('l', 1, 1, 0, 4)
-        density(0, 1, 0, 0)
-        density(0, 1, 0, 2)
-        overlap_interleave(1, 0, 1, 'dve')
-        density(0, 1, 0, 1)
-        turn_out('l', 1, 0, 0, 'dve')
-        density_out(0, 1, 0, 2, 'act')
-        load_orbitals('r', 1, 0, 0, 4)
-        density(0, 1, 0, 3)
-        turn('l', 1, 1, 0)
-        turn('l', 1, 1, 1)
-        quantise(('r', 1, 1))
-        turn('r', 1, 0, 0)
-        density_out(0, 1, 0, 0, 'act')
-        density_out(0, 1, 0, 1, 'act')
-        load_overlap(0, 0)
-        turn('r', 1, 0, 1)
-        quantise(('l', 1, 0))
-        turn_out('l', 1, 1, 0, 'dve')
-        density_out(0, 1, 0, 3, 'act')
-        overlap_interleave(0, 0, 1, 'dve')
-        load_orbitals('r', 0, 0, 0, 2)
-        density(1, 1, 0, 1)
-        overlap_interleave(0, 0, 0, 'act')
-        density(1, 1, 0, 0)
-        load_orbitals('l', 0, 1, 0, 4)
-        turn_out('l', 1, 1, 1, 'dve')
-        turn_out('r', 1, 0, 1, 'act')
-        quantise(('s', 1, 0))
         load_orbitals('r', 0, 0, 2, 2)
-        turn_out('r', 1, 0, 0, 'act')
-        density_out(1, 1, 0, 1, 'act')
-        turn('r', 0, 0, 0)
-        density_out(1, 1, 0, 0, 'dve')
-        quantise(('l', 1, 1))
+        load_orbitals('l', 0, 0, 2, 2)
         turn('r', 0, 0, 1)
-        turn('l', 0, 1, 1)
-        turn_out('r', 0, 0, 0, 'act')
-        quantise(('r', 1, 0))
-        turn('l', 0, 1, 0)
-        density(1, 1, 1, 0)
-        density(1, 1, 0, 2)
-        density(1, 0, 0, 2)
-        turn_out('l', 0, 1, 1, 'dve')
         turn_out('r', 0, 0, 1, 'act')
-        turn_out('l', 0, 1, 0, 'dve')
-        density(1, 1, 0, 3)
-        density_out(1, 1, 1, 0, 'act')
-        density_out(1, 1, 0, 2, 'act')
+        turn('l', 0, 0, 1)
+        load_orbitals('l', 0, 0, 0, 2)
+        load_orbitals('r', 0, 0, 0, 2)
+        turn('l', 0, 0, 0)
+        turn_out('l', 0, 0, 1, 'dve')
+        load_orbitals('r', 0, 1, 0, 4)
+        turn('r', 0, 0, 0)
+        load_orbitals('l', 1, 0, 0, 4)
+        turn_out('r', 0, 0, 0, 'act')
+        turn('r', 0, 1, 0)
+        turn_out('r', 0, 1, 0, 'act')
+        load_overlap(0, 0)
+        turn_out('l', 0, 0, 0, 'dve')
+        turn('r', 0, 1, 1)
+        turn_out('r', 0, 1, 1, 'act')
+        quantise(('l', 0, 0))
+        turn('l', 1, 0, 0)
         quantise(('r', 0, 0))
-        quantise(('l', 0, 1))
-        density_out(1, 1, 0, 3, 'act')
-        density(1, 0, 0, 0)
-        density_out(1, 0, 0, 2, 'dve')
-        density(1, 0, 0, 1)
-        density(1, 0, 0, 3)
-        density(1, 0, 1, 1)
-        density_out(1, 0, 0, 0, 'act')
-        density_out(1, 0, 0, 1, 'act')
-        density_out(1, 0, 1, 1, 'act')
-        density_out(1, 0, 0, 3, 'dve')
-        quantise(('s', 0, 0))
-        density(0, 0, 1, 2)
-        load_overlap(1, 1)
         density(0, 0, 0, 0)
-        quantise(('p', 1, 0, 0))
+        turn_out('l', 1, 0, 0, 'dve')
+        quantise(('r', 0, 1))
         density(0, 0, 0, 1)
-        density(1, 0, 1, 3)
-        density(1, 1, 1, 3)
-        density_out(0, 0, 1, 2, 'act')
-        quantise(('p', 1, 1, 0))
-        density_out(0, 0, 0, 0, 'act')
-        density(0, 0, 0, 3)
-        load_overlap(0, 1)
-        density(1, 1, 1, 2)
+        turn('l', 1, 0, 1)
         density(0, 0, 0, 2)
+        load_orbitals('l', 0, 1, 0, 4)
+        density_out(0, 0, 0, 0, 'act')
+        density(0, 1, 0, 3)
+        overlap_interleave(0, 0, 1, 'dve')
+        overlap_interleave(0, 0, 0, 'dve')
+        turn_out('l', 1, 0, 1, 'dve')
+        load_orbitals('r', 1, 1, 0, 4)
+        density(0, 0, 0, 3)
+        density(0, 1, 0, 2)
+        turn('l', 0, 1, 1)
+        load_orbitals('r', 1, 0, 0, 4)
+        quantise(('s', 0, 0))
         density_out(0, 0, 0, 1, 'act')
-        density(0, 1, 1, 3)
-        density_out(1, 1, 1, 3, 'dve')
-        density_out(1, 0, 1, 3, 'act')
-        density_out(0, 0, 0, 2, 'dve')
-        direct_product(1, (0, 0, 0))
-        direct_product(1, (0, 0, 1))
-        density(1, 0, 1, 2)
-        overlap_interleave(1, 1, 0, 'dve')
+        overlap_interleave(0, 1, 1, 'act')
+        turn('l', 0, 1, 0)
+        turn_out('l', 0, 1, 1, 'dve')
+        turn_out('l', 0, 1, 0, 'dve')
+        density_out(0, 1, 0, 3, 'act')
+        density_out(0, 0, 0, 2, 'act')
+        turn('r', 1, 1, 0)
         density_out(0, 0, 0, 3, 'act')
-        density(0, 0, 1, 0)
-        quantise(('p', 0, 1, 0))
-        mirror_product(1, (0, 0, 1))
-        density_out(1, 1, 1, 2, 'act')
+        load_orbitals('l', 1, 1, 0, 4)
         quantise(('p', 0, 0, 0))
-        density(1, 0, 1, 0)
-        density_out(0, 1, 1, 3, 'act')
-        density(1, 1, 1, 1)
-        overlap_interleave(0, 1, 0, 'dve')
-        direct_out(1, (0, 0, 0))
-        direct_out(1, (0, 0, 1))
-        overlap_interleave(0, 1, 1, 'dve')
-        density_out(1, 0, 1, 2, 'act')
-        density_out(0, 0, 1, 0, 'act')
-        multiply(1, (0, 0, 1))
-        density_out(1, 0, 1, 0, 'act')
-        direct_product(0, (0, 0, 0))
-        density_out(1, 1, 1, 1, 'act')
-        direct_product(0, (0, 0, 1))
-        overlap_interleave(1, 1, 1, 'dve')
-        quantise(('s', 0, 1))
-        mirror_product(1, (0, 0, 0))
-        density(0, 1, 1, 0)
-        quantise(('s', 1, 1))
-        direct_product(0, (0, 0, 2))
-        mirror_product(0, (0, 0, 1))
-        direct_out(0, (0, 0, 1))
-        direct_out(0, (0, 0, 0))
-        mirror_product(0, (0, 0, 2))
-        density(0, 0, 1, 3)
-        quantise(('p', 1, 1, 1))
-        multiply(1, (0, 0, 0))
-        direct_product(0, (0, 1, 2))
-        direct_out(0, (0, 0, 2))
-        density(0, 1, 1, 2)
-        mirror_product(0, (0, 0, 0))
-        density_out(0, 1, 1, 0, 'act')
-        direct_out(0, (0, 1, 2))
+        quantise(('l', 0, 1))
+        turn('r', 1, 1, 1)
+        density_out(0, 1, 0, 2, 'act')
+        turn('r', 1, 0, 0)
+        quantise(('l', 1, 0))
+        turn('r', 1, 0, 1)
+        turn('l', 1, 1, 1)
+        turn_out('r', 1, 1, 0, 'act')
+        turn_out('r', 1, 0, 0, 'act')
+        turn_out('r', 1, 1, 1, 'act')
+        turn_out('r', 1, 0, 1, 'act')
+        turn_out('l', 1, 1, 1, 'dve')
+        quantise(('r', 1, 1))
+        quantise(('r', 1, 0))
+        density(0, 1, 0, 1)
         density(0, 0, 1, 1)
-        density_out(0, 1, 1, 2, 'act')
-        multiply(0, (0, 0, 1))
-        multiply(0, (0, 0, 2))
-        quantise(('p', 1, 0, 1))
-        multiply(0, (0, 0, 0))
-        add_channels((0, 0, 1), 'dve')
-        density_out(0, 0, 1, 3, 'act')
+        turn('l', 1, 1, 0)
+        load_overlap(1, 0)
+        density(0, 1, 0, 0)
+        density_out(0, 1, 0, 1, 'act')
         density_out(0, 0, 1, 1, 'act')
-        direct_product(1, (0, 1, 0))
+        density_out(0, 1, 0, 0, 'act')
+        density(0, 0, 1, 3)
+        density_out(0, 0, 1, 3, 'act')
+        density(1, 1, 0, 1)
+        density(1, 0, 0, 0)
+        turn_out('l', 1, 1, 0, 'dve')
+        density_out(1, 0, 0, 0, 'act')
+        density(1, 0, 0, 3)
+        density_out(1, 1, 0, 1, 'act')
+        density(1, 0, 0, 1)
+        density(0, 1, 1, 0)
+        density_out(1, 0, 0, 3, 'act')
+        density_out(1, 0, 0, 1, 'act')
         density(0, 1, 1, 1)
-        direct_product(0, (0, 1, 3))
-        add_channels((0, 0, 0), 'dve')
-        add_channels((0, 0, 2), 'dve')
-        quantise(('p', 0, 0, 1))
-        direct_out(1, (0, 1, 0))
-        direct_product(1, (0, 1, 3))
-        direct_product(1, (0, 1, 2))
+        density(1, 0, 0, 2)
+        density_out(0, 1, 1, 0, 'act')
+        overlap_interleave(1, 0, 0, 'dve')
+        overlap_interleave(1, 0, 1, 'dve')
         density_out(0, 1, 1, 1, 'act')
+        density(1, 1, 0, 2)
+        quantise(('p', 0, 1, 0))
+        quantise(('s', 1, 0))
+        density(1, 1, 0, 0)
+        density(0, 1, 1, 3)
+        density(1, 1, 0, 3)
+        direct_product(0, (0, 0, 1))
+        quantise(('l', 1, 1))
+        direct_product(0, (0, 0, 0))
+        density(1, 0, 1, 2)
+        density_out(1, 1, 0, 0, 'dve')
+        density_out(1, 0, 0, 2, 'dve')
+        density_out(1, 1, 0, 3, 'dve')
+        quantise(('p', 1, 0, 0))
+        density_out(1, 1, 0, 2, 'act')
+        density(1, 0, 1, 3)
+        overlap_interleave(1, 1, 1, 'dve')
+        density(0, 0, 1, 0)
+        density_out(0, 1, 1, 3, 'act')
+        direct_out(0, (0, 0, 0))
+        mirror_product(0, (0, 0, 0))
+        direct_out(0, (0, 0, 1))
+        density(0, 1, 1, 2)
+        mirror_product(0, (0, 0, 1))
+        density_out(1, 0, 1, 2, 'act')
+        density_out(1, 0, 1, 3, 'act')
+        quantise(('p', 1, 1, 0))
+        multiply(0, (0, 0, 0))
+        density_out(0, 0, 1, 0, 'act')
+        density_out(0, 1, 1, 2, 'act')
+        density(0, 0, 1, 2)
+        density(1, 0, 1, 1)
+        mirror_product(0, (0, 0, 2))
+        density_out(0, 0, 1, 2, 'act')
+        overlap_interleave(1, 1, 0, 'dve')
+        overlap_interleave(0, 1, 0, 'dve')
+        direct_product(0, (0, 0, 2))
+        direct_out(0, (0, 0, 2))
+        density_out(1, 0, 1, 1, 'act')
+        multiply(0, (0, 0, 1))
+        quantise(('s', 1, 1))
+        quantise(('s', 0, 1))
+        density(1, 1, 1, 0)
+        mirror_product(1, (0, 0, 1))
+        direct_product(1, (0, 0, 1))
+        multiply(0, (0, 0, 2))
         quantise(('p', 0, 1, 1))
-        mirror_rows(0, 0, 1)
-        mirror_out(0, 0, 1, 'dve')
-        mirror_rows(0, 0, 3)
-        direct_out(1, (0, 1, 3))
-        mirror_out(0, 0, 3, 'dve')
-        direct_out(1, (0, 1, 2))
-        order_row(0, 0, 0, 'act')
-        mirror_product(1, (0, 1, 0))
-        mirror_product(1, (0, 1, 2))
-        direct_product(0, (0, 1, 0))
-        direct_out(0, (0, 1, 3))
-        order_row(0, 0, 2, 'dve')
-        order_row(0, 0, 1, 'act')
-        mirror_product(0, (0, 1, 2))
-        multiply(1, (0, 1, 2))
-        mirror_product(1, (0, 1, 3))
-        direct_out(0, (0, 1, 0))
-        multiply(1, (0, 1, 0))
-        mirror_product(0, (0, 1, 3))
-        mirror_product(0, (0, 1, 0))
-        round_result(0, 0, 0, 'act')
-        multiply(0, (0, 1, 2))
-        multiply(1, (0, 1, 3))
-        multiply(0, (0, 1, 3))
-        direct_product(0, (0, 1, 1))
-        round_result(0, 0, 1, 'act')
-        multiply(0, (0, 1, 0))
-        direct_out(0, (0, 1, 1))
+        mirror_product(1, (0, 0, 0))
+        direct_product(1, (0, 0, 0))
+        direct_out(1, (0, 0, 1))
+        density_out(1, 1, 1, 0, 'act')
+        density(1, 1, 1, 1)
+        density(1, 1, 1, 2)
+        direct_product(0, (0, 1, 2))
+        multiply(1, (0, 0, 1))
+        direct_out(1, (0, 0, 0))
+        multiply(1, (0, 0, 0))
+        density_out(1, 1, 1, 2, 'act')
+        direct_out(0, (0, 1, 2))
+        density(1, 0, 1, 0)
+        density(1, 1, 1, 3)
+        add_channels((0, 0, 2), 'dve')
+        add_channels((0, 0, 1), 'dve')
+        add_channels((0, 0, 0), 'dve')
         direct_product(1, (0, 1, 1))
-        add_channels((0, 1, 3), 'dve')
-        mirror_product(0, (0, 1, 1))
-        add_channels((0, 1, 2), 'dve')
+        density_out(1, 0, 1, 0, 'act')
+        density_out(1, 1, 1, 1, 'act')
+        density_out(1, 1, 1, 3, 'act')
+        direct_product(0, (0, 1, 1))
+        direct_product(1, (0, 1, 2))
+        quantise(('p', 0, 0, 1))
+        mirror_rows(0, 0, 1)
         direct_out(1, (0, 1, 1))
+        mirror_rows(0, 0, 3)
+        mirror_product(0, (0, 1, 2))
+        direct_product(1, (0, 1, 3))
+        mirror_product(0, (0, 1, 1))
+        direct_out(0, (0, 1, 1))
+        mirror_out(0, 0, 1, 'act')
+        order_row(0, 0, 0, 'dve')
+        quantise(('p', 1, 0, 1))
+        quantise(('p', 1, 1, 1))
         mirror_product(1, (0, 1, 1))
+        multiply(0, (0, 1, 2))
+        order_row(0, 0, 2, 'dve')
+        order_row(0, 0, 1, 'dve')
+        mirror_out(0, 0, 3, 'act')
         multiply(0, (0, 1, 1))
-        store_rows(0, 0, 0, 1)
-        direct_product(0, (1, 1, 1))
-        direct_product(1, (1, 1, 0))
+        direct_out(1, (0, 1, 2))
+        direct_out(1, (0, 1, 3))
+        mirror_product(1, (0, 1, 2))
+        round_result(0, 0, 0, 'act')
+        direct_product(0, (0, 1, 0))
+        mirror_product(1, (0, 1, 3))
         multiply(1, (0, 1, 1))
-        add_channels((0, 1, 0), 'dve')
+        multiply(1, (0, 1, 2))
+        direct_product(0, (0, 1, 3))
+        direct_out(0, (0, 1, 0))
+        direct_product(1, (0, 1, 0))
+        mirror_product(0, (0, 1, 3))
         add_channels((0, 1, 1), 'dve')
-        order_row(0, 1, 3, 'act')
-        store_rows(0, 1, 3, 1)
-        direct_product(0, (1, 1, 0))
-        order_row(0, 1, 0, 'dve')
-        mirror_product(0, (1, 1, 0))
+        multiply(1, (0, 1, 3))
+        quantise_result(0, 0, 0)
+        direct_out(0, (0, 1, 3))
+        order_row(0, 1, 1, 'dve')
+        multiply(0, (0, 1, 3))
+        add_channels((0, 1, 2), 'dve')
+        direct_out(1, (0, 1, 0))
+        round_result(0, 0, 1, 'act')
+        mirror_product(0, (0, 1, 0))
         direct_product(1, (1, 1, 1))
-        direct_out(0, (1, 1, 1))
-        mirror_product(0, (1, 1, 1))
-        direct_out(1, (1, 1, 0))
-        direct_out(0, (1, 1, 0))
-        mirror_product(1, (1, 1, 1))
+        multiply(0, (0, 1, 0))
+        store_rows(0, 0, 0, 1)
         store_rows(0, 0, 1, 1)
-        order_row(0, 1, 2, 'dve')
-        order_row(0, 1, 1, 'act')
-        quantise_result(0, 0)
-        mirror_product(1, (1, 1, 0))
+        store_rows(0, 0, 2, 1)
+        direct_product(1, (1, 1, 0))
         direct_out(1, (1, 1, 1))
-        multiply(0, (1, 1, 0))
-        multiply(0, (1, 1, 1))
-        mirror_product(0, (1, 1, 2))
+        mirror_product(1, (0, 1, 0))
+        mirror_product(0, (1, 1, 0))
+        direct_out(1, (1, 1, 0))
+        add_channels((0, 1, 3), 'dve')
+        multiply(1, (0, 1, 0))
+        direct_product(0, (1, 1, 0))
         direct_product(0, (1, 1, 2))
-        mirror_rows(1, 0, 1)
-        mirror_rows(1, 0, 2)
-        multiply(1, (1, 1, 1))
+        order_row(0, 1, 3, 'act')
+        quantise_result(0, 0, 1)
+        add_channels((0, 1, 0), 'dve')
+        order_row(0, 1, 2, 'dve')
+        store_rows(0, 0, 3, 1)
+        direct_out(0, (1, 1, 0))
+        store_rows(0, 1, 1, 1)
+        store_words(0, 0)
+        store_rows(0, 1, 2, 1)
+        direct_out(0, (1, 1, 2))
+        direct_product(0, (1, 1, 1))
+        direct_out(0, (1, 1, 1))
+        mirror_product(1, (1, 1, 0))
+        mirror_product(1, (1, 1, 1))
+        order_row(0, 1, 0, 'dve')
+        multiply(0, (1, 1, 0))
         round_result(0, 1, 0, 'act')
         multiply(1, (1, 1, 0))
-        store_rows(0, 0, 3, 1)
-        round_result(0, 1, 1, 'act')
-        add_channels((1, 1, 1), 'dve')
-        store_words(0, 0)
+        multiply(1, (1, 1, 1))
         add_channels((1, 1, 0), 'dve')
-        mirror_rows(1, 0, 0)
-        store_rows(0, 1, 2, 1)
-        mirror_rows(1, 1, 1)
-        store_rows(0, 0, 2, 1)
-        direct_out(0, (1, 1, 2))
-        mirror_out(1, 0, 1, 'act')
-        store_rows(0, 1, 1, 1)
-        quantise_result(0, 1)
-        store_rows(0, 1, 0, 1)
-        store_words(0, 1)
-        mirror_rows(1, 0, 3)
-        mirror_out(1, 0, 0, 'act')
+        mirror_rows(1, 0, 2)
+        mirror_product(0, (1, 1, 1))
+        mirror_product(0, (1, 1, 2))
+        mirror_out(1, 0, 2, 'act')
+        order_row(1, 1, 0, 'act')
+        multiply(0, (1, 1, 1))
         multiply(0, (1, 1, 2))
-        mirror_out(1, 0, 2, 'dve')
-        store_rows(1, 0, 1, 1)
+        store_rows(0, 1, 0, 1)
+        store_rows(0, 1, 3, 1)
+        add_channels((1, 1, 1), 'dve')
+        mirror_rows(1, 0, 1)
         add_channels((1, 1, 2), 'dve')
-        mirror_out(1, 1, 1, 'act')
-        store_rows(1, 0, 0, 1)
-        order_row(1, 1, 0, 'dve')
-        mirror_out(1, 0, 3, 'act')
-        order_row(1, 1, 1, 'act')
-        mirror_rows(1, 1, 3)
+        mirror_rows(1, 0, 0)
+        mirror_out(1, 0, 1, 'act')
+        quantise_result(0, 1, 0)
+        round_result(0, 1, 1, 'dve')
+        mirror_out(1, 0, 0, 'act')
         store_rows(1, 0, 2, 1)
-        store_scales(0)
-        order_row(1, 1, 2, 'dve')
-        store_rows(1, 0, 3, 1)
-        round_result(1, 0, 1, 'dve')
-        round_result(1, 0, 0, 'dve')
+        mirror_rows(1, 0, 3)
+        mirror_rows(1, 1, 1)
+        mirror_out(1, 0, 3, 'act')
         store_rows(1, 1, 0, 1)
-        store_rows(1, 1, 1, 1)
+        mirror_out(1, 1, 1, 'act')
+        store_rows(1, 0, 1, 1)
+        store_rows(1, 0, 0, 1)
+        store_rows(1, 0, 3, 1)
+        mirror_rows(1, 1, 3)
         mirror_out(1, 1, 3, 'act')
-        store_rows(1, 1, 2, 1)
-        round_result(1, 1, 0, 'dve')
-        round_result(1, 1, 1, 'act')
+        round_result(1, 0, 0, 'dve')
+        order_row(1, 1, 1, 'act')
+        order_row(1, 1, 2, 'dve')
         store_rows(1, 1, 3, 1)
-        quantise_result(1, 0)
-        quantise_result(1, 1)
+        quantise_result(0, 1, 1)
+        round_result(1, 0, 1, 'dve')
+        store_rows(1, 1, 2, 1)
+        store_words(0, 1)
+        round_result(1, 1, 0, 'act')
+        store_scales(0)
+        quantise_result(1, 0, 0)
+        store_rows(1, 1, 1, 1)
+        quantise_result(1, 0, 1)
+        round_result(1, 1, 1, 'dve')
+        quantise_result(1, 1, 0)
+        quantise_result(1, 1, 1)
         store_words(1, 0)
         store_words(1, 1)
         store_scales(1)

from contextlib import ExitStack

import concourse.mybir as mybir
from concourse.masks import make_identity

T, N, O = 2, 1024, 512
FLOPS = 2 * T * (N * N * O + N * N * N)

F32 = mybir.dt.float32
BF16 = mybir.dt.bfloat16
U32 = mybir.dt.uint32
I32 = mybir.dt.int32
U8 = mybir.dt.uint8
FP8X4 = mybir.dt.float8_e4m3fn_x4
MULT = mybir.AluOpType.mult
ADD = mybir.AluOpType.add

P = 128
PACK = 4
GROUP = P * PACK
G = N // GROUP


def tile_biorthogonalspinmayerbondorder_x1_kernel(tc, l, r, occ, s, out_0, out_1, out_2):
    nc = tc.nc
    with ExitStack() as ctx:
        keep = ctx.enter_context(tc.tile_pool(name="keep", bufs=1))
        work = ctx.enter_context(tc.tile_pool(name="work", bufs=4))
        psum = ctx.enter_context(tc.psum_pool(name="psum", bufs=8))
        ctx.enter_context(tc.manual_schedule())

        raw, staged, quantised, banks, products, result, summed = {}, {}, {}, {}, {}, {}, {}

        def bank(key):
            banks[key] = psum.tile([P, GROUP], F32, name="bank")
            return banks[key]

        def copier(engine):
            return nc.scalar.copy if engine == "act" else nc.vector.tensor_copy

        def load_orbitals(which, t, g, j0, step):
            src = (l if which == "l" else r)[t, g * GROUP : (g + 1) * GROUP, :].rearrange("(m j) k -> m j k", j=PACK)
            piece = keep.tile([P, step, O], BF16, name="raw_%s%d%d%d" % (which, t, g, j0))
            nc.sync.dma_start(out=piece[:], in_=src[:, j0 : j0 + step, :])
            for j in range(step):
                raw[which, t, g, j0 + j] = piece[:, j, :]

        def load_overlap(h, g):
            piece = keep.tile([P, PACK, N], BF16, name="raw_s%d" % h)
            nc.sync.dma_start(out=piece[:], in_=s[h * GROUP : (h + 1) * GROUP, :].rearrange("(p j) d -> p j d", j=PACK))
            raw["s", h] = piece

        def stage(key):
            if key not in staged:
                staged[key] = work.tile([P, GROUP * PACK], BF16, name="staged", align_bytes=64, bufs=9)
            return staged[key]

        def turn(which, t, g, half):
            dst = bank((which, t, g, half))
            for j2 in range(2):
                words = raw[which, t, g, 2 * half + j2].bitcast(F32)
                for u in range(2):
                    at = (2 * u + j2) * P
                    nc.tensor.transpose(dst[:, at : at + P], words[:, u::2], ident[:])

        def turn_out(which, t, g, half, engine):
            src = banks[which, t, g, half]
            dst = stage((which, t, g))[:, half * 2 * GROUP : (half + 1) * 2 * GROUP]
            if which == "r":
                copier(engine)(
                    out=dst.bitcast(F32).rearrange("p (c u) -> p c u", u=2),
                    in_=src[:].rearrange("p (u c) -> p c u", u=2),
                )
            else:
                nc.vector.tensor_tensor(
                    out=dst.rearrange("p (c u e) -> p c u e", u=2, e=2),
                    in0=src[:].bitcast(BF16).rearrange("p (u c e) -> p c u e", u=2, e=2),
                    in1=occ_sb[:, t, :].rearrange("p (u e) -> p u e", u=2).unsqueeze(1).to_broadcast([P, 2 * P, 2, 2]),
                    op=MULT,
                )

        def quantise(key):
            name = "_".join(str(part) for part in key)
            codes = keep.tile([P, GROUP], U32, name="codes_" + name, align_bytes=64)
            scales = keep.tile([P, GROUP], U8, name="scales_" + name, align_bytes=64)
            nc.vector.quantize_mx(out=codes[:].bitcast(FP8X4), scales=scales[:], in_=staged[key][:])
            quantised[key] = (codes, scales)

        def mx(dst, left, left_cols, right, right_cols, start, stop):
            nc.tensor.matmul_mx(
                out=dst,
                lhsT=quantised[left][0][:, left_cols].bitcast(FP8X4),
                lhsT_scale=quantised[left][1][:, left_cols],
                rhs=quantised[right][0][:, right_cols].bitcast(FP8X4),
                rhs_scale=quantised[right][1][:, right_cols],
                start=start,
                stop=stop,
            )

        def block(j, count=1):
            return slice(j * P, (j + count) * P)

        def density(t, h, g, c):
            dst = bank(("p", t, h, g, c))
            for j in range(PACK):
                mx(dst[:, block(j)], ("r", t, h), block(j), ("l", t, g), block(c), True, True)

        def density_out(t, h, g, c, engine):
            dst = stage(("p", t, h, g))[:, c * GROUP : (c + 1) * GROUP]
            copier(engine)(
                out=dst.rearrange("p (m j) -> p m j", j=PACK),
                in_=banks["p", t, h, g, c][:].rearrange("p (j m) -> p m j", j=PACK),
            )

        def overlap_interleave(h, g, half, engine):
            pairs = slice(half * P // 4, (half + 1) * P // 4)
            dst = stage(("s", h, g))[:].rearrange("p (c q e j) -> p q c e j", c=PACK, e=2, j=PACK)[:, pairs]
            src = raw["s", h][:, :, g * GROUP : (g + 1) * GROUP].rearrange("p j (q e c) -> p q c e j", e=2, c=PACK)[:, pairs]
            if engine == "pool":
                nc.gpsimd.tensor_scalar(out=dst, in0=src, scalar1=1.0, scalar2=0.0, op0=MULT, op1=ADD)
            else:
                copier(engine)(out=dst, in_=src)

        def pieces_of(t, unit):
            g, g2, j = unit
            if g != g2 or j == 0:
                return [(t, j, block(0, 4), block(0, 4))]
            if j == 1:
                return [(t, 1, block(0, 2), block(1, 2)), (t, 1, block(2), block(3)), (t, 3, block(3), block(3))]
            return [(t2, 2, block(2 * t2, 2), block(2, 2)) for t2 in range(T)]

        def direct_product(t, unit):
            g, g2, _ = unit
            direct = bank(("x", t, unit))
            for t2, j, at, cols in pieces_of(t, unit):
                for h in range(G):
                    mx(direct[:, at], ("p", t2, h, g), block(j), ("s", h, g2), cols, h == 0, h == G - 1)

        def mirror_product(t, unit):
            g, g2, _ = unit
            mirror = bank(("y", t, unit))
            for t2, j, at, cols in pieces_of(t, unit):
                for h in range(G):
                    mx(mirror[:, at], ("s", h, g), block(j), ("p", t2, h, g2), cols, h == 0, h == G - 1)

        def direct_out(t, unit):
            staged["x", t, unit] = work.tile([P, GROUP], F32, name="direct", bufs=6)
            nc.scalar.copy(out=staged["x", t, unit][:], in_=banks["x", t, unit][:])

        def multiply(t, unit):
            products[t, unit] = work.tile([P, GROUP], F32, name="product", bufs=10)
            nc.vector.scalar_tensor_tensor(
                out=products[t, unit][:], in0=banks["y", t, unit][:], scalar=2.0, in1=staged["x", t, unit][:], op0=MULT, op1=MULT
            )

        def quadrant(g, g2):
            if (g, g2) not in result:
                result[g, g2] = keep.tile([P, PACK, GROUP], F32, name="result_%d%d" % (g, g2))
            return result[g, g2]

        def sums(g, g2):
            if (g, g2) not in summed:
                summed[g, g2] = keep.tile([P, (13 if g == g2 else 16) * P], F32, name="sums_%d%d" % (g, g2))
            return summed[g, g2]

        def place(g, g2, j, c):
            if g != g2:
                return PACK * j + c
            return {0: 0, 1: 4, 2: 9, 3: 5}[j] + c

        def add_channels(unit, engine):
            g, g2, j = unit
            if g == g2 and j == 2:
                dst = block(place(g, g, 2, 2), 2)
                first, second = products[0, unit][:, block(0, 2)], products[0, unit][:, block(2, 2)]
            else:
                dst = block(place(g, g2, j, j if g == g2 else 0), 4)
                first, second = products[0, unit][:], products[1, unit][:]
            (nc.vector if engine == "dve" else nc.gpsimd).tensor_tensor(out=sums(g, g2)[:, dst], in0=first, in1=second, op=ADD)

        def mirror_rows(g, g2, j):
            dst = bank(("m", g, g2, j))
            wanted = [(1, 0), (2, 0), (2, 1)] if (g == g2 and j == 1) else [(j, c) for c in range(PACK)]
            for at, (row, c) in enumerate(wanted):
                nc.tensor.transpose(dst[:, block(at)], sums(g2, g)[:, block(place(g2, g, c, row))], ident[:])

        def mirror_out(g, g2, j, engine):
            src = banks["m", g, g2, j]
            if g == g2 and j == 1:
                copier(engine)(out=sums(g, g)[:, block(place(g, g, 1, 0))], in_=src[:, block(0)])
                copier(engine)(out=sums(g, g)[:, block(place(g, g, 2, 0), 2)], in_=src[:, block(1, 2)])
            else:
                copier(engine)(
                    out=quadrant(g, g2)[:, j, :].rearrange("p (q c) -> p q c", c=PACK),
                    in_=src[:].rearrange("p (c q) -> p q c", c=PACK),
                )

        def order_row(g, g2, j, engine):
            copier(engine)(
                out=quadrant(g, g2)[:, j, :].rearrange("p (q c) -> p q c", c=PACK),
                in_=sums(g, g2)[:, block(place(g, g2, j, 0), 4)].rearrange("p (c q) -> p q c", c=PACK),
            )

        def store_rows(g, g2, j0, count):
            rows = out_0[g * GROUP : (g + 1) * GROUP, g2 * GROUP : (g2 + 1) * GROUP].rearrange("(p j) m -> p j m", j=PACK)
            nc.sync.dma_start(out=rows[:, j0 : j0 + count, :], in_=result[g, g2][:, j0 : j0 + count, :])

        def round_result(g, g2, half, engine):
            m = slice(half * 2 * P, (half + 1) * 2 * P)
            copier(engine)(
                out=stage(("o", g, g2))[:].rearrange("p (m j) -> p m j", j=PACK)[:, m, :],
                in_=result[g, g2][:].rearrange("p j m -> p m j")[:, m, :],
            )

        def quantise_result(g, g2, half):
            if ("o", g, g2) not in quantised:
                quantised["o", g, g2] = keep.tile([P, GROUP], U32, name="out_codes_%d%d" % (g, g2), align_bytes=64)
            nc.vector.quantize_mx(
                out=quantised["o", g, g2][:, block(2 * half, 2)].bitcast(FP8X4),
                scales=out_scales[g][:, block(PACK * g2 + 2 * half, 2)],
                in_=staged["o", g, g2][:, half * 2 * GROUP : (half + 1) * 2 * GROUP],
            )

        def store_words(g, g2):
            words = out_1[g].rearrange("p m j -> p (m j)").bitcast(I32)
            nc.sync.dma_start(out=words[:, g2 * GROUP : (g2 + 1) * GROUP], in_=quantised["o", g, g2][:].bitcast(I32))

        def store_scales(g):
            for q in range(4):
                nc.sync.dma_start(
                    out=out_2[g, 4 * q : 4 * q + 4, :].bitcast(I32), in_=out_scales[g][32 * q : 32 * q + 4, :].bitcast(I32)
                )

        ident = keep.tile([P, P], F32, name="ident")
        make_identity(nc, ident[:])
        occ_sb = keep.tile([P, T, PACK], BF16, name="occ_sb")
        nc.scalar.dma_start(out=occ_sb[:], in_=occ.rearrange("t (p j) -> p t j", j=PACK))
        out_scales = [keep.tile([P, N], U8, name="out_scales_%d" % g, align_bytes=64) for g in range(G)]

        load_orbitals('r', 0, 0, 2, 2)
        load_orbitals('l', 0, 0, 2, 2)
        turn('r', 0, 0, 1)
        turn_out('r', 0, 0, 1, 'act')
        turn('l', 0, 0, 1)
        load_orbitals('l', 0, 0, 0, 2)
        load_orbitals('r', 0, 0, 0, 2)
        turn('l', 0, 0, 0)
        turn_out('l', 0, 0, 1, 'dve')
        load_orbitals('r', 0, 1, 0, 4)
        turn('r', 0, 0, 0)
        load_orbitals('l', 1, 0, 0, 4)
        turn_out('r', 0, 0, 0, 'act')
        turn('r', 0, 1, 0)
        turn_out('r', 0, 1, 0, 'act')
        load_overlap(0, 0)
        turn_out('l', 0, 0, 0, 'dve')
        turn('r', 0, 1, 1)
        turn_out('r', 0, 1, 1, 'act')
        quantise(('l', 0, 0))
        turn('l', 1, 0, 0)
        quantise(('r', 0, 0))
        density(0, 0, 0, 0)
        turn_out('l', 1, 0, 0, 'dve')
        quantise(('r', 0, 1))
        density(0, 0, 0, 1)
        turn('l', 1, 0, 1)
        density(0, 0, 0, 2)
        load_orbitals('l', 0, 1, 0, 4)
        density_out(0, 0, 0, 0, 'act')
        density(0, 1, 0, 3)
        overlap_interleave(0, 0, 1, 'dve')
        overlap_interleave(0, 0, 0, 'dve')
        turn_out('l', 1, 0, 1, 'dve')
        load_orbitals('r', 1, 1, 0, 4)
        density(0, 0, 0, 3)
        density(0, 1, 0, 2)
        turn('l', 0, 1, 1)
        load_orbitals('r', 1, 0, 0, 4)
        quantise(('s', 0, 0))
        density_out(0, 0, 0, 1, 'act')
        overlap_interleave(0, 1, 1, 'act')
        turn('l', 0, 1, 0)
        turn_out('l', 0, 1, 1, 'dve')
        turn_out('l', 0, 1, 0, 'dve')
        density_out(0, 1, 0, 3, 'act')
        density_out(0, 0, 0, 2, 'act')
        turn('r', 1, 1, 0)
        density_out(0, 0, 0, 3, 'act')
        load_orbitals('l', 1, 1, 0, 4)
        quantise(('p', 0, 0, 0))
        quantise(('l', 0, 1))
        turn('r', 1, 1, 1)
        density_out(0, 1, 0, 2, 'act')
        turn('r', 1, 0, 0)
        quantise(('l', 1, 0))
        turn('r', 1, 0, 1)
        turn('l', 1, 1, 1)
        turn_out('r', 1, 1, 0, 'act')
        turn_out('r', 1, 0, 0, 'act')
        turn_out('r', 1, 1, 1, 'act')
        turn_out('r', 1, 0, 1, 'act')
        turn_out('l', 1, 1, 1, 'dve')
        quantise(('r', 1, 1))
        quantise(('r', 1, 0))
        density(0, 1, 0, 1)
        density(0, 0, 1, 1)
        turn('l', 1, 1, 0)
        load_overlap(1, 0)
        density(0, 1, 0, 0)
        density_out(0, 1, 0, 1, 'act')
        density_out(0, 0, 1, 1, 'act')
        density_out(0, 1, 0, 0, 'act')
        density(0, 0, 1, 3)
        density_out(0, 0, 1, 3, 'act')
        density(1, 1, 0, 1)
        density(1, 0, 0, 0)
        turn_out('l', 1, 1, 0, 'dve')
        density_out(1, 0, 0, 0, 'act')
        density(1, 0, 0, 3)
        density_out(1, 1, 0, 1, 'act')
        density(1, 0, 0, 1)
        density(0, 1, 1, 0)
        density_out(1, 0, 0, 3, 'act')
        density_out(1, 0, 0, 1, 'act')
        density(0, 1, 1, 1)
        density(1, 0, 0, 2)
        density_out(0, 1, 1, 0, 'act')
        overlap_interleave(1, 0, 0, 'dve')
        overlap_interleave(1, 0, 1, 'dve')
        density_out(0, 1, 1, 1, 'act')
        density(1, 1, 0, 2)
        quantise(('p', 0, 1, 0))
        quantise(('s', 1, 0))
        density(1, 1, 0, 0)
        density(0, 1, 1, 3)
        density(1, 1, 0, 3)
        direct_product(0, (0, 0, 1))
        quantise(('l', 1, 1))
        direct_product(0, (0, 0, 0))
        density(1, 0, 1, 2)
        density_out(1, 1, 0, 0, 'dve')
        density_out(1, 0, 0, 2, 'dve')
        density_out(1, 1, 0, 3, 'dve')
        quantise(('p', 1, 0, 0))
        density_out(1, 1, 0, 2, 'act')
        density(1, 0, 1, 3)
        overlap_interleave(1, 1, 1, 'dve')
        density(0, 0, 1, 0)
        density_out(0, 1, 1, 3, 'act')
        direct_out(0, (0, 0, 0))
        mirror_product(0, (0, 0, 0))
        direct_out(0, (0, 0, 1))
        density(0, 1, 1, 2)
        mirror_product(0, (0, 0, 1))
        density_out(1, 0, 1, 2, 'act')
        density_out(1, 0, 1, 3, 'act')
        quantise(('p', 1, 1, 0))
        multiply(0, (0, 0, 0))
        density_out(0, 0, 1, 0, 'act')
        density_out(0, 1, 1, 2, 'act')
        density(0, 0, 1, 2)
        density(1, 0, 1, 1)
        mirror_product(0, (0, 0, 2))
        density_out(0, 0, 1, 2, 'act')
        overlap_interleave(1, 1, 0, 'dve')
        overlap_interleave(0, 1, 0, 'dve')
        direct_product(0, (0, 0, 2))
        direct_out(0, (0, 0, 2))
        density_out(1, 0, 1, 1, 'act')
        multiply(0, (0, 0, 1))
        quantise(('s', 1, 1))
        quantise(('s', 0, 1))
        density(1, 1, 1, 0)
        mirror_product(1, (0, 0, 1))
        direct_product(1, (0, 0, 1))
        multiply(0, (0, 0, 2))
        quantise(('p', 0, 1, 1))
        mirror_product(1, (0, 0, 0))
        direct_product(1, (0, 0, 0))
        direct_out(1, (0, 0, 1))
        density_out(1, 1, 1, 0, 'act')
        density(1, 1, 1, 1)
        density(1, 1, 1, 2)
        direct_product(0, (0, 1, 2))
        multiply(1, (0, 0, 1))
        direct_out(1, (0, 0, 0))
        multiply(1, (0, 0, 0))
        density_out(1, 1, 1, 2, 'act')
        direct_out(0, (0, 1, 2))
        density(1, 0, 1, 0)
        density(1, 1, 1, 3)
        add_channels((0, 0, 2), 'dve')
        add_channels((0, 0, 1), 'dve')
        add_channels((0, 0, 0), 'dve')
        direct_product(1, (0, 1, 1))
        density_out(1, 0, 1, 0, 'act')
        density_out(1, 1, 1, 1, 'act')
        density_out(1, 1, 1, 3, 'act')
        direct_product(0, (0, 1, 1))
        direct_product(1, (0, 1, 2))
        quantise(('p', 0, 0, 1))
        mirror_rows(0, 0, 1)
        direct_out(1, (0, 1, 1))
        mirror_rows(0, 0, 3)
        mirror_product(0, (0, 1, 2))
        direct_product(1, (0, 1, 3))
        mirror_product(0, (0, 1, 1))
        direct_out(0, (0, 1, 1))
        mirror_out(0, 0, 1, 'act')
        order_row(0, 0, 0, 'dve')
        quantise(('p', 1, 0, 1))
        quantise(('p', 1, 1, 1))
        mirror_product(1, (0, 1, 1))
        multiply(0, (0, 1, 2))
        order_row(0, 0, 2, 'dve')
        order_row(0, 0, 1, 'dve')
        mirror_out(0, 0, 3, 'act')
        multiply(0, (0, 1, 1))
        direct_out(1, (0, 1, 2))
        direct_out(1, (0, 1, 3))
        mirror_product(1, (0, 1, 2))
        round_result(0, 0, 0, 'act')
        direct_product(0, (0, 1, 0))
        mirror_product(1, (0, 1, 3))
        multiply(1, (0, 1, 1))
        multiply(1, (0, 1, 2))
        direct_product(0, (0, 1, 3))
        direct_out(0, (0, 1, 0))
        direct_product(1, (0, 1, 0))
        mirror_product(0, (0, 1, 3))
        add_channels((0, 1, 1), 'dve')
        multiply(1, (0, 1, 3))
        quantise_result(0, 0, 0)
        direct_out(0, (0, 1, 3))
        order_row(0, 1, 1, 'dve')
        multiply(0, (0, 1, 3))
        add_channels((0, 1, 2), 'dve')
        direct_out(1, (0, 1, 0))
        round_result(0, 0, 1, 'act')
        mirror_product(0, (0, 1, 0))
        direct_product(1, (1, 1, 1))
        multiply(0, (0, 1, 0))
        store_rows(0, 0, 0, 1)
        store_rows(0, 0, 1, 1)
        store_rows(0, 0, 2, 1)
        direct_product(1, (1, 1, 0))
        direct_out(1, (1, 1, 1))
        mirror_product(1, (0, 1, 0))
        mirror_product(0, (1, 1, 0))
        direct_out(1, (1, 1, 0))
        add_channels((0, 1, 3), 'dve')
        multiply(1, (0, 1, 0))
        direct_product(0, (1, 1, 0))
        direct_product(0, (1, 1, 2))
        order_row(0, 1, 3, 'act')
        quantise_result(0, 0, 1)
        add_channels((0, 1, 0), 'dve')
        order_row(0, 1, 2, 'dve')
        store_rows(0, 0, 3, 1)
        direct_out(0, (1, 1, 0))
        store_rows(0, 1, 1, 1)
        store_words(0, 0)
        store_rows(0, 1, 2, 1)
        direct_out(0, (1, 1, 2))
        direct_product(0, (1, 1, 1))
        direct_out(0, (1, 1, 1))
        mirror_product(1, (1, 1, 0))
        mirror_product(1, (1, 1, 1))
        order_row(0, 1, 0, 'dve')
        multiply(0, (1, 1, 0))
        round_result(0, 1, 0, 'act')
        multiply(1, (1, 1, 0))
        multiply(1, (1, 1, 1))
        add_channels((1, 1, 0), 'dve')
        mirror_rows(1, 0, 2)
        mirror_product(0, (1, 1, 1))
        mirror_product(0, (1, 1, 2))
        mirror_out(1, 0, 2, 'act')
        order_row(1, 1, 0, 'act')
        multiply(0, (1, 1, 1))
        multiply(0, (1, 1, 2))
        store_rows(0, 1, 0, 1)
        store_rows(0, 1, 3, 1)
        add_channels((1, 1, 1), 'dve')
        mirror_rows(1, 0, 1)
        add_channels((1, 1, 2), 'dve')
        mirror_rows(1, 0, 0)
        mirror_out(1, 0, 1, 'act')
        quantise_result(0, 1, 0)
        round_result(0, 1, 1, 'dve')
        mirror_out(1, 0, 0, 'act')
        store_rows(1, 0, 2, 1)
        mirror_rows(1, 0, 3)
        mirror_rows(1, 1, 1)
        mirror_out(1, 0, 3, 'act')
        store_rows(1, 1, 0, 1)
        mirror_out(1, 1, 1, 'act')
        store_rows(1, 0, 1, 1)
        store_rows(1, 0, 0, 1)
        store_rows(1, 0, 3, 1)
        mirror_rows(1, 1, 3)
        mirror_out(1, 1, 3, 'act')
        round_result(1, 0, 0, 'dve')
        order_row(1, 1, 1, 'act')
        order_row(1, 1, 2, 'dve')
        store_rows(1, 1, 3, 1)
        quantise_result(0, 1, 1)
        round_result(1, 0, 1, 'dve')
        store_rows(1, 1, 2, 1)
        store_words(0, 1)
        round_result(1, 1, 0, 'act')
        store_scales(0)
        quantise_result(1, 0, 0)
        store_rows(1, 1, 1, 1)
        quantise_result(1, 0, 1)
        round_result(1, 1, 1, 'dve')
        quantise_result(1, 1, 0)
        quantise_result(1, 1, 1)
        store_words(1, 0)
        store_words(1, 1)
        store_scales(1)
